import numpy as np
import ml_dtypes


def mxq(x, axis, fmt="e4m3"):
    dtype, down = {"e4m3": (ml_dtypes.float8_e4m3fn, 7), "e5m2": (ml_dtypes.float8_e5m2, 14)}[fmt]
    v = np.moveaxis(np.asarray(x, np.float32).astype(ml_dtypes.bfloat16).astype(np.float64), axis, -1)
    blocks = v.reshape(v.shape[:-1] + (-1, 32))
    amax = np.abs(blocks).max(-1, keepdims=True)
    byte = np.maximum(np.where(amax > 0, np.frexp(amax)[1] - 1 + 127, 0) - down, 1)
    scale = np.exp2(byte - 127.0)
    codes = (blocks / scale).astype(np.float32).astype(dtype).astype(np.float64)
    return np.moveaxis((codes * scale).reshape(v.shape), -1, axis)


WIDE = False


def mx_kscale(k):
    if not WIDE:
        return np.ones(k)
    levels = np.array([10, -10, 5, -5, 0])
    if k % 512:
        return np.exp2(np.random.permutation(np.resize(levels, k // 32))).repeat(32)
    a = np.empty((k // 512, 16))
    for p in range(k // 512):
        a[p, :8] = np.random.permutation(np.resize(levels, 8))
        for g in range(8):
            far = levels[np.abs(levels - a[p, g]) >= 10]
            a[p, g + 8] = far[np.random.randint(len(far))]
    return np.exp2(a.ravel()).repeat(32)


def f64(x):
    return np.asarray(x).astype(np.float64)


def striped(idx):
    return np.tile(idx.reshape(-1, 16).T, (8, 1)).astype(np.uint16)


def unstriped(offs):
    return offs[:16].T.reshape(-1).astype(np.int64)


def pack_weight(w):
    k, n = w.shape
    w = f64(np.asarray(w, np.float32).astype(ml_dtypes.bfloat16)).reshape(k // 32, 32, n)
    amax = np.abs(w).max(1)
    byte = np.clip(np.where(amax > 0, np.frexp(amax)[1] - 1 + 127 - 7, 1), 1, 254)
    scaled = (w * np.exp2(127.0 - byte)[:, None, :]).reshape(k, n).astype(np.float32)
    words = np.ascontiguousarray(scaled.reshape(k // 512, 128, 4, n).transpose(0, 1, 3, 2)).astype(ml_dtypes.float8_e4m3fn).view(np.uint8)
    return words, np.ascontiguousarray(byte.astype(np.uint8).reshape(k // 512, 16, n))


def unpack_weight(words, scales):
    g, p, n, _ = words.shape
    vals = np.ascontiguousarray(words).view(ml_dtypes.float8_e4m3fn).astype(np.float64) * np.repeat(np.exp2(scales.astype(np.float64) - 127.0), 8, axis=1)[..., None]
    return vals.transpose(0, 1, 3, 2).reshape(g * 512, n)


E2M1 = np.array([0.0, 0.5, 1.0, 1.5, 2.0, 3.0, 4.0, 6.0, -0.0, -0.5, -1.0, -1.5, -2.0, -3.0, -4.0, -6.0])


def pack_fp4(w):
    k, n = w.shape
    w = f64(np.asarray(w, np.float32).astype(ml_dtypes.bfloat16)).reshape(k // 32, 32, n)
    amax = np.abs(w).max(1)
    mant, ex = np.frexp(amax / 6.0)
    byte = np.clip(np.where(amax > 0, np.where(mant > 0.5, ex, ex - 1) + 127, 1), 1, 254)
    scaled = (w * np.exp2(127.0 - byte)[:, None, :]).reshape(k, n).astype(np.float32)
    c = np.ascontiguousarray(scaled.reshape(k // 512, 128, 4, n).transpose(0, 1, 3, 2)).astype(ml_dtypes.float4_e2m1fn).view(np.uint8) & 0xF
    words = (c[..., 0::2] | (c[..., 1::2] << 4)).reshape(k // 512, 128, 2 * n)
    return np.ascontiguousarray(words), np.ascontiguousarray(byte.astype(np.uint8).reshape(k // 512, 16, n))


def unpack_fp4(words, scales):
    g, _, n = scales.shape
    words = np.ascontiguousarray(words).reshape(g, 128, n, 2)
    nib = np.empty((g, 128, n, 4), np.uint8)
    nib[..., 0::2] = words & 0xF
    nib[..., 1::2] = words >> 4
    vals = E2M1[nib] * np.repeat(np.exp2(scales.astype(np.float64) - 127.0), 8, axis=1)[..., None]
    return vals.transpose(0, 1, 3, 2).reshape(g * 512, n)


K, T, S, N, H = 512, 1024, 512, 256, 512


def setup_inputs():
    n = np.random.standard_normal
    s = mx_kscale(K)[:, None]
    u = mx_kscale(H)
    packed_xT = pack_weight(n((K, T)) * s)
    packed_w1 = pack_fp4(n((K, H)) / np.sqrt(K) / s)
    packed_w2 = pack_fp4(n((H, N)) / np.sqrt(H) / u[:, None])
    return {
        "x_words": packed_xT[0],
        "x_scales": packed_xT[1],
        "w1_words": packed_w1[0],
        "w1_scales": packed_w1[1],
        "unit": (np.random.uniform(0.6, 1.4, (H, 1)) * u[:, None]).astype(np.float32),
        "w2_words": packed_w2[0],
        "w2_scales": packed_w2[1],
        "offs": striped(np.random.permutation(T)[:S]),
        "h1": striped(np.random.permutation(S)),
        "h2": striped(np.random.permutation(S)),
        "h3": striped(np.random.permutation(S)),
    }


def reference(x_words, x_scales, w1_words, w1_scales, unit, w2_words, w2_scales, offs, h1, h2, h3):
    xq = unpack_weight(x_words, x_scales)[:, unstriped(offs)]
    uu = unpack_fp4(w1_words, w1_scales).T @ xq
    heat = np.exp(0.8 * np.tanh(uu))
    a1 = heat[:, unstriped(h1)]
    gx = a1 - heat
    a2 = heat[:, unstriped(h2)]
    gy = a2 - heat
    nrm = np.sqrt((gx) ** 2 + (gy) ** 2 + 0.05)
    vx = gx / nrm
    xb = vx[:, unstriped(h3)]
    vy = gy / nrm
    yb = vy[:, unstriped(h3)]
    div_ = vx - xb + vy - yb
    hid = f64(unit) * (div_ * heat - (0.5 * vx))
    return unpack_fp4(w2_words, w2_scales).T @ mxq(hid, 0, "e4m3")

@@ -1,0 +1,234 @@
+from contextlib import ExitStack
+
+import concourse.mybir as mybir
+from concourse.masks import make_identity
+
+K, T, S, N, H = 512, 1024, 512, 256, 512
+FLOPS = 2 * K * H * S + 2 * H * N * S
+
+F32 = mybir.dt.float32
+BF16 = mybir.dt.bfloat16
+I32 = mybir.dt.int32
+U32 = mybir.dt.uint32
+U16 = mybir.dt.uint16
+U8 = mybir.dt.uint8
+FP8X4 = mybir.dt.float8_e4m3fn_x4
+FP4X4 = mybir.dt.float4_e2m1fn_x4
+ACT = mybir.ActivationFunctionType
+ALU = mybir.AluOpType
+
+P = 128
+PACK = 4
+HALF = S // 2
+CHUNKS = ((0, 256), (256, 128), (384, 128))
+
+
+def load_scale_rows(queue, plane, rows):
+    for q in range(4):
+        queue.dma_start(out=plane[32 * q : 32 * q + 4, :].bitcast(I32), in_=rows[4 * q : 4 * q + 4, :].bitcast(I32))
+
+
+def tile_picked_yheatg_mul_p_kernel(tc, x_words, x_scales, w1_words, w1_scales, unit, w2_words, w2_scales, offs, h1, h2, h3, out):
+    nc = tc.nc
+    with ExitStack() as ctx:
+        keep = ctx.enter_context(tc.tile_pool(name="keep", bufs=1))
+        ring = ctx.enter_context(tc.tile_pool(name="ring", bufs=2))
+        psum = ctx.enter_context(tc.psum_pool(name="psum", bufs=2))
+
+        offs_sb = keep.tile([P, S // 16], U16, name="offs_sb")
+        h1_sb = keep.tile([P, S // 16], U16, name="h1_sb")
+        h2_sb = keep.tile([P, S // 16], U16, name="h2_sb")
+        h3_sb = keep.tile([P, S // 16], U16, name="h3_sb")
+        xw = keep.tile([P, T], U32, name="xw", align_bytes=64)
+        xs = keep.tile([P, T], U8, name="xs", align_bytes=64)
+        w1w = keep.tile([P, 2 * H], U8, name="w1w", align_bytes=64)
+        w1s = keep.tile([P, H], U8, name="w1s", align_bytes=64)
+        w2w = keep.tile([P, 2 * N], U8, name="w2w", align_bytes=64)
+        w2s = keep.tile([P, N], U8, name="w2s", align_bytes=64)
+        unit_sb = keep.tile([P, PACK], F32, name="unit_sb")
+        ident = keep.tile([P, P], F32, name="ident")
+
+        nc.gpsimd.memset(xs[:].bitcast(I32), 0)
+        nc.gpsimd.memset(w1s[:].bitcast(I32), 0)
+        nc.gpsimd.memset(w2s[:].bitcast(I32), 0)
+
+        nc.sync.dma_start(offs_sb[:], offs)
+        nc.sync.dma_start(out=w1w[:].bitcast(I32), in_=w1_words[0].bitcast(I32))
+        nc.sync.dma_start(out=xw[:].bitcast(I32), in_=x_words[0].rearrange("p n t -> p (n t)").bitcast(I32))
+        load_scale_rows(nc.sync, xs, x_scales[0])
+        load_scale_rows(nc.sync, w1s, w1_scales[0])
+        nc.sync.dma_start(out=unit_sb[:], in_=unit.rearrange("(p t) o -> p (t o)", t=PACK))
+        nc.sync.dma_start(h1_sb[:], h1)
+        nc.sync.dma_start(h2_sb[:], h2)
+        nc.sync.dma_start(h3_sb[:], h3)
+        nc.sync.dma_start(out=w2w[:].bitcast(I32), in_=w2_words[0].bitcast(I32))
+        load_scale_rows(nc.sync, w2s, w2_scales[0])
+        make_identity(nc, ident[:])
+
+        half_unit = keep.tile([P, PACK], F32, name="half_unit")
+        nc.scalar.activation(half_unit[:], unit_sb[:], ACT.Copy, scale=0.25)
+
+        w1w_dealt = keep.tile([P, 2 * H], U8, name="w1w_dealt", align_bytes=64)
+        w1s_dealt = keep.tile([P, H], U8, name="w1s_dealt", align_bytes=64)
+        nc.vector.tensor_copy(
+            out=w1w_dealt[:].rearrange("p (t m b) -> p t m b", t=PACK, b=2),
+            in_=w1w[:].rearrange("p (m t b) -> p t m b", t=PACK, b=2),
+        )
+        xg_s = keep.tile([P, S], U8, name="xg_s", align_bytes=64)
+        xg_w = keep.tile([P, S], U32, name="xg_w", align_bytes=64)
+        nc.vector.tensor_copy(xg_s[:], xs[:].indirect(offs_sb[:]))
+        nc.vector.tensor_copy(
+            out=w1s_dealt[:].rearrange("p (t m) -> p t m", t=PACK),
+            in_=w1s[:].rearrange("p (m t) -> p t m", t=PACK),
+        )
+        nc.vector.tensor_copy(xg_w[:], xw[:].indirect(offs_sb[:]))
+
+        heat_win = [keep.tile([P, 2 * S], F32, name=f"heat_win{t}") for t in range(PACK)]
+        heat = [keep.tile([P, S], F32, name=f"heat{t}") for t in range(PACK)]
+        grad = [keep.tile([P, 2, S], F32, name=f"grad{t}") for t in range(PACK)]
+        gsum = [keep.tile([P, S], F32, name=f"gsum{t}") for t in range(PACK)]
+        vsum = [keep.tile([P, S], F32, name=f"vsum{t}") for t in range(PACK)]
+        term_div = keep.tile([P, PACK, S], F32, name="term_div")
+        term_vx = keep.tile([P, PACK, S], F32, name="term_vx")
+
+        for t in range(PACK):
+            uu = psum.tile([P, S], F32, name="uu", tag="mm")
+            nc.tensor.matmul_mx(
+                out=uu[:],
+                lhsT=w1w_dealt[:, 2 * P * t : 2 * P * (t + 1)].bitcast(FP4X4),
+                lhsT_scale=w1s_dealt[:, P * t : P * (t + 1)],
+                rhs=xg_w[:].bitcast(FP8X4),
+                rhs_scale=xg_s[:],
+                start=True,
+                stop=True,
+            )
+            nc.scalar.activation(heat_win[t][:, S:], uu[:], ACT.Tanh)
+            nc.scalar.activation(heat_win[t][:, :S], heat_win[t][:, S:], ACT.Exp, scale=0.8)
+            if t == 0:
+                nc.vector.tensor_copy(heat[t][:], heat_win[t][:, :S])
+            else:
+                nc.sync.dma_start(out=heat[t][:], in_=heat_win[t][:, :S])
+
+        inv_norm = []
+        newton = []
+        near = []
+
+        def gradients(t):
+            nc.vector.tensor_tensor(grad[t][:, 0, :], heat_win[t][:].indirect(h1_sb[:]), heat[t][:], ALU.subtract)
+            nc.vector.tensor_tensor(grad[t][:, 1, :], heat_win[t][:].indirect(h2_sb[:]), heat[t][:], ALU.subtract)
+
+        def norm(t):
+            squares = ring.tile([P, 2, S], F32, name="squares")
+            nc.scalar.activation(squares[:], grad[t][:], ACT.Square)
+            sum_t = psum.tile([P, S], F32, name="sum_t", tag="sum_t")
+            for j in range(PACK):
+                cols = slice(P * j, P * (j + 1))
+                nc.tensor.matmul(sum_t[:, cols], squares[:, 0, cols], ident[:], start=True, stop=False, is_transpose=True)
+                nc.tensor.matmul(sum_t[:, cols], squares[:, 1, cols], ident[:], start=False, stop=True, is_transpose=True)
+            guess = ring.tile([P, S], F32, name="guess")
+            nc.scalar.activation(guess[:], sum_t[:], ACT.Abs_reciprocal_sqrt, bias=0.05)
+            guess_sq = ring.tile([P, S], F32, name="guess_sq")
+            nc.scalar.activation(guess_sq[:], guess[:], ACT.Square)
+            newton.append((sum_t, guess, guess_sq))
+
+        def polish_a(t):
+            sum_t, guess, guess_sq = newton[t]
+            near_one = ring.tile([P, S], F32, name="near_one")
+            nc.vector.scalar_tensor_tensor(near_one[:], sum_t[:], 0.05, guess_sq[:], ALU.add, ALU.mult)
+            near.append(near_one)
+
+        def polish_b(t):
+            guess = newton[t][1]
+            inv_t = ring.tile([P, S], F32, name="inv_t")
+            nc.vector.scalar_tensor_tensor(inv_t[:], near[t][:], -3.0, guess[:], ALU.add, ALU.mult)
+            inv = psum.tile([P, S], F32, name="inv", tag="inv", bufs=4)
+            for j in range(PACK):
+                cols = slice(P * j, P * (j + 1))
+                nc.tensor.transpose(inv[:, cols], inv_t[:, cols], ident[:])
+            inv_norm.append(inv)
+
+        def gradient_sum(t):
+            nc.vector.tensor_tensor(gsum[t][:], grad[t][:, 0, :], grad[t][:, 1, :], ALU.add)
+
+        fetched = []
+
+        def normalise(t):
+            nc.vector.scalar_tensor_tensor(vsum[t][:], gsum[t][:], -0.5, inv_norm[t][:], ALU.mult, ALU.mult)
+            nc.vector.scalar_tensor_tensor(
+                term_vx[:, t, :], grad[t][:, 0, :], half_unit[:, t : t + 1], inv_norm[t][:], ALU.mult, ALU.mult
+            )
+            got = ring.tile([P, S], F32, name="got")
+            for a in range(2):
+                nc.scalar.activation(
+                    got[:, HALF * a : HALF * (a + 1)], vsum[t][:].indirect(h3_sb[:, 16 * a : 16 * (a + 1)]), ACT.Copy
+                )
+            fetched.append(got)
+
+        def divergence(t):
+            div = ring.tile([P, S], F32, name="div")
+            nc.vector.tensor_tensor(div[:], vsum[t][:], fetched[t][:], ALU.subtract)
+            return div
+
+        def weigh(t, div):
+            nc.vector.scalar_tensor_tensor(term_div[:, t, :], div[:], unit_sb[:, t : t + 1], heat[t][:], ALU.mult, ALU.mult)
+
+        gradients(0)
+        norm(0)
+        gradients(1)
+        norm(1)
+        gradient_sum(0)
+        gradients(2)
+        gradient_sum(1)
+        polish_a(0)
+        gradient_sum(2)
+        polish_b(0)
+        norm(2)
+        gradients(3)
+        polish_a(1)
+        gradient_sum(3)
+        polish_b(1)
+        norm(3)
+        normalise(0)
+        normalise(1)
+        polish_a(2)
+        div = divergence(0)
+        polish_b(2)
+        weigh(0, div)
+        polish_a(3)
+        div = divergence(1)
+        polish_b(3)
+        weigh(1, div)
+        normalise(2)
+        normalise(3)
+        div2 = divergence(2)
+        weigh(2, div2)
+        div3 = divergence(3)
+        weigh(3, div3)
+
+        out_v = out.rearrange("(m p) n -> p m n", p=P)
+        for c0, width in CHUNKS:
+            cols = slice(c0, c0 + width)
+            hid = keep.tile([P, width, PACK], BF16, name=f"hid{c0}", align_bytes=64)
+            nc.vector.tensor_tensor(
+                hid[:].rearrange("p (c i) t -> p c t i", i=4),
+                term_div[:, :, cols].rearrange("p t (c i) -> p c t i", i=4),
+                term_vx[:, :, cols].rearrange("p t (c i) -> p c t i", i=4),
+                ALU.add,
+            )
+            codes = keep.tile([P, width], U32, name=f"codes{c0}", align_bytes=64)
+            scales = keep.tile([P, width], U8, name=f"scales{c0}", align_bytes=64)
+            nc.vector.quantize_mx(out=codes[:].bitcast(FP8X4), scales=scales[:], in_=hid[:].rearrange("p n t -> p (n t)"))
+            acc = psum.tile([P, 2, width], F32, name="acc", tag="mm")
+            for m in range(2):
+                nc.tensor.matmul_mx(
+                    out=acc[:, m, :],
+                    lhsT=w2w[:, 2 * P * m : 2 * P * (m + 1)].bitcast(FP4X4),
+                    lhsT_scale=w2s[:, P * m : P * (m + 1)],
+                    rhs=codes[:].bitcast(FP8X4),
+                    rhs_scale=scales[:],
+                    start=True,
+                    stop=True,
+                )
+            res = keep.tile([P, 2, width], F32, name=f"res{c0}")
+            nc.scalar.copy(res[:], acc[:])
+            nc.sync.dma_start(out=out_v[:, :, cols], in_=res[:])

@@ -23,16 +23,23 @@ HALF = S // 2
 CHUNKS = ((0, 256), (256, 128), (384, 128))
 
 
-def load_scale_rows(queue, plane, rows):
-    for q in range(4):
+def load_scale_rows(queue, plane, rows, quadrants):
+    for q in quadrants:
         queue.dma_start(out=plane[32 * q : 32 * q + 4, :].bitcast(I32), in_=rows[4 * q : 4 * q + 4, :].bitcast(I32))
+
+
+def load_scale_rows_repeated(queue, plane, rows, quadrants):
+    width = rows.shape[1] // 4
+    for q in quadrants:
+        four = rows[4 * q : 4 * q + 4, :].bitcast(I32)
+        queue.dma_start(out=plane[32 * q : 32 * q + 32, :].bitcast(I32), in_=four.unsqueeze(0).to_broadcast([8, 4, width]))
 
 
 def tile_picked_yheatg_mul_p_kernel(tc, x_words, x_scales, w1_words, w1_scales, unit, w2_words, w2_scales, offs, h1, h2, h3, out):
     nc = tc.nc
     with ExitStack() as ctx:
         keep = ctx.enter_context(tc.tile_pool(name="keep", bufs=1))
-        ring = ctx.enter_context(tc.tile_pool(name="ring", bufs=2))
+        ring = ctx.enter_context(tc.tile_pool(name="ring", bufs=PACK))
         psum = ctx.enter_context(tc.psum_pool(name="psum", bufs=2))
 
         offs_sb = keep.tile([P, S // 16], U16, name="offs_sb")
@@ -42,171 +49,208 @@ def tile_picked_yheatg_mul_p_kernel(tc, x_words, x_scales, w1_words, w1_scales, 
         xw = keep.tile([P, T], U32, name="xw", align_bytes=64)
         xs = keep.tile([P, T], U8, name="xs", align_bytes=64)
         w1w = keep.tile([P, 2 * H], U8, name="w1w", align_bytes=64)
-        w1s = keep.tile([P, H], U8, name="w1s", align_bytes=64)
+        w1s = keep.tile([P, H], U8, name="w1s", tag="w1_bytes", align_bytes=64)
         w2w = keep.tile([P, 2 * N], U8, name="w2w", align_bytes=64)
         w2s = keep.tile([P, N], U8, name="w2s", align_bytes=64)
         unit_sb = keep.tile([P, PACK], F32, name="unit_sb")
         ident = keep.tile([P, P], F32, name="ident")
 
-        nc.gpsimd.memset(xs[:].bitcast(I32), 0)
-        nc.gpsimd.memset(w1s[:].bitcast(I32), 0)
         nc.gpsimd.memset(w2s[:].bitcast(I32), 0)
 
         nc.sync.dma_start(offs_sb[:], offs)
+        load_scale_rows_repeated(nc.sync, xs, x_scales[0], range(4))
         nc.sync.dma_start(out=w1w[:].bitcast(I32), in_=w1_words[0].bitcast(I32))
         nc.sync.dma_start(out=xw[:].bitcast(I32), in_=x_words[0].rearrange("p n t -> p (n t)").bitcast(I32))
-        load_scale_rows(nc.sync, xs, x_scales[0])
-        load_scale_rows(nc.sync, w1s, w1_scales[0])
-        nc.sync.dma_start(out=unit_sb[:], in_=unit.rearrange("(p t) o -> p (t o)", t=PACK))
+        load_scale_rows_repeated(nc.sync, w1s, w1_scales[0], range(4))
         nc.sync.dma_start(h1_sb[:], h1)
         nc.sync.dma_start(h2_sb[:], h2)
+        nc.sync.dma_start(out=unit_sb[:], in_=unit.rearrange("(p t) o -> p (t o)", t=PACK))
         nc.sync.dma_start(h3_sb[:], h3)
         nc.sync.dma_start(out=w2w[:].bitcast(I32), in_=w2_words[0].bitcast(I32))
-        load_scale_rows(nc.sync, w2s, w2_scales[0])
+        load_scale_rows(nc.sync, w2s, w2_scales[0], range(4))
         make_identity(nc, ident[:])
 
-        half_unit = keep.tile([P, PACK], F32, name="half_unit")
-        nc.scalar.activation(half_unit[:], unit_sb[:], ACT.Copy, scale=0.25)
+        quarter_unit = keep.tile([P, PACK], F32, name="quarter_unit")
+        nc.gpsimd.tensor_scalar(quarter_unit[:], unit_sb[:], 0.25, 0.0, ALU.mult, ALU.add)
 
-        w1w_dealt = keep.tile([P, 2 * H], U8, name="w1w_dealt", align_bytes=64)
-        w1s_dealt = keep.tile([P, H], U8, name="w1s_dealt", align_bytes=64)
-        nc.vector.tensor_copy(
-            out=w1w_dealt[:].rearrange("p (t m b) -> p t m b", t=PACK, b=2),
-            in_=w1w[:].rearrange("p (m t b) -> p t m b", t=PACK, b=2),
-        )
+        w1w_first = keep.tile([P, 2 * P], U8, name="w1w_first", align_bytes=64)
+        w1s_dealt = keep.tile([P, PACK, P], U8, name="w1s_dealt", align_bytes=64)
+        w1w_by_tile = w1w[:].rearrange("p (m t b) -> p t m b", t=PACK, b=2)
+
+        def deal_scales(tiles):
+            nc.vector.tensor_copy(out=w1s_dealt[:, tiles, :], in_=w1s[:].rearrange("p (m t) -> p t m", t=PACK)[:, tiles])
+
         xg_s = keep.tile([P, S], U8, name="xg_s", align_bytes=64)
         xg_w = keep.tile([P, S], U32, name="xg_w", align_bytes=64)
+        halves = [slice(0, HALF), slice(HALF, S)]
+        list_halves = [slice(0, HALF // 16), slice(HALF // 16, S // 16)]
         nc.vector.tensor_copy(xg_s[:], xs[:].indirect(offs_sb[:]))
-        nc.vector.tensor_copy(
-            out=w1s_dealt[:].rearrange("p (t m) -> p t m", t=PACK),
-            in_=w1s[:].rearrange("p (m t) -> p t m", t=PACK),
-        )
-        nc.vector.tensor_copy(xg_w[:], xw[:].indirect(offs_sb[:]))
+        nc.vector.tensor_copy(out=w1w_first[:].rearrange("p (m b) -> p m b", b=2), in_=w1w_by_tile[:, 0])
+        nc.vector.tensor_copy(xg_w[:, halves[0]], xw[:].indirect(offs_sb[:, list_halves[0]]))
+        deal_scales(slice(0, 1))
+        nc.vector.tensor_copy(xg_w[:, halves[1]], xw[:].indirect(offs_sb[:, list_halves[1]]))
+        deal_scales(slice(1, PACK))
+        w1w_rest = keep.tile([P, PACK - 1, 2 * P], U8, name="w1w_rest", tag="w1_bytes", align_bytes=64)
+        nc.vector.tensor_copy(out=w1w_rest[:].rearrange("p t (m b) -> p t m b", b=2), in_=w1w_by_tile[:, 1:])
+        w1_tiles = [w1w_first[:]] + [w1w_rest[:, t, :] for t in range(PACK - 1)]
 
         heat_win = [keep.tile([P, 2 * S], F32, name=f"heat_win{t}") for t in range(PACK)]
         heat = [keep.tile([P, S], F32, name=f"heat{t}") for t in range(PACK)]
         grad = [keep.tile([P, 2, S], F32, name=f"grad{t}") for t in range(PACK)]
-        gsum = [keep.tile([P, S], F32, name=f"gsum{t}") for t in range(PACK)]
-        vsum = [keep.tile([P, S], F32, name=f"vsum{t}") for t in range(PACK)]
         term_div = keep.tile([P, PACK, S], F32, name="term_div")
         term_vx = keep.tile([P, PACK, S], F32, name="term_vx")
 
         for t in range(PACK):
-            uu = psum.tile([P, S], F32, name="uu", tag="mm")
-            nc.tensor.matmul_mx(
-                out=uu[:],
-                lhsT=w1w_dealt[:, 2 * P * t : 2 * P * (t + 1)].bitcast(FP4X4),
-                lhsT_scale=w1s_dealt[:, P * t : P * (t + 1)],
-                rhs=xg_w[:].bitcast(FP8X4),
-                rhs_scale=xg_s[:],
-                start=True,
-                stop=True,
-            )
-            nc.scalar.activation(heat_win[t][:, S:], uu[:], ACT.Tanh)
-            nc.scalar.activation(heat_win[t][:, :S], heat_win[t][:, S:], ACT.Exp, scale=0.8)
-            if t == 0:
-                nc.vector.tensor_copy(heat[t][:], heat_win[t][:, :S])
-            else:
-                nc.sync.dma_start(out=heat[t][:], in_=heat_win[t][:, :S])
+            for cols in halves if t == 0 else [slice(0, S)]:
+                width = cols.stop - cols.start
+                uu = psum.tile([P, width], F32, name="uu", tag="mm")
+                nc.tensor.matmul_mx(
+                    out=uu[:],
+                    lhsT=w1_tiles[t].bitcast(FP4X4),
+                    lhsT_scale=w1s_dealt[:, t, :],
+                    rhs=xg_w[:, cols].bitcast(FP8X4),
+                    rhs_scale=xg_s[:, cols],
+                    start=True,
+                    stop=True,
+                )
+                tanh_cols = slice(S + cols.start, S + cols.stop)
+                nc.scalar.activation(heat_win[t][:, tanh_cols], uu[:], ACT.Tanh)
+                nc.scalar.activation(heat_win[t][:, cols], heat_win[t][:, tanh_cols], ACT.Exp, scale=0.8)
+                if t < 2:
+                    nc.vector.tensor_copy(heat[t][:, cols], heat_win[t][:, cols])
+                else:
+                    nc.sync.dma_start(out=heat[t][:], in_=heat_win[t][:, :S])
 
-        inv_norm = []
-        newton = []
-        near = []
-
-        def gradients(t):
-            nc.vector.tensor_tensor(grad[t][:, 0, :], heat_win[t][:].indirect(h1_sb[:]), heat[t][:], ALU.subtract)
-            nc.vector.tensor_tensor(grad[t][:, 1, :], heat_win[t][:].indirect(h2_sb[:]), heat[t][:], ALU.subtract)
-
-        def norm(t):
-            squares = ring.tile([P, 2, S], F32, name="squares")
-            nc.scalar.activation(squares[:], grad[t][:], ACT.Square)
-            sum_t = psum.tile([P, S], F32, name="sum_t", tag="sum_t")
+        def turn(bank, parts):
             for j in range(PACK):
                 cols = slice(P * j, P * (j + 1))
-                nc.tensor.matmul(sum_t[:, cols], squares[:, 0, cols], ident[:], start=True, stop=False, is_transpose=True)
-                nc.tensor.matmul(sum_t[:, cols], squares[:, 1, cols], ident[:], start=False, stop=True, is_transpose=True)
+                for i, part in enumerate(parts):
+                    nc.tensor.matmul(
+                        bank[:, cols], part[:, cols], ident[:], start=(i == 0), stop=(i == len(parts) - 1), is_transpose=True
+                    )
+
+        st = [{} for t in range(PACK)]
+
+        def gradient(t, axis):
+            neighbours = (h1_sb, h2_sb)[axis]
+            nc.vector.tensor_tensor(grad[t][:, axis, :], heat_win[t][:].indirect(neighbours[:]), heat[t][:], ALU.subtract)
+
+        def square(t):
+            squares = keep.tile([P, 2, S], F32, name="squares", tag=f"squares{max(t, 1)}")
+            nc.scalar.activation(squares[:], grad[t][:], ACT.Square)
+            sq_sum = psum.tile([P, S], F32, name="sq_sum", tag="sq_sum")
+            turn(sq_sum, [squares[:, 0, :], squares[:, 1, :]])
+            st[t]["sq_sum"] = sq_sum
+
+        def guess_root(t):
             guess = ring.tile([P, S], F32, name="guess")
-            nc.scalar.activation(guess[:], sum_t[:], ACT.Abs_reciprocal_sqrt, bias=0.05)
+            nc.scalar.activation(guess[:], st[t]["sq_sum"][:], ACT.Abs_reciprocal_sqrt, bias=0.05)
             guess_sq = ring.tile([P, S], F32, name="guess_sq")
             nc.scalar.activation(guess_sq[:], guess[:], ACT.Square)
-            newton.append((sum_t, guess, guess_sq))
+            st[t]["guess"] = guess
+            st[t]["guess_sq"] = guess_sq
+            g_sum = psum.tile([P, S], F32, name="g_sum", tag="g_sum")
+            turn(g_sum, [grad[t][:, 0, :], grad[t][:, 1, :]])
+            st[t]["g_sum"] = g_sum
 
-        def polish_a(t):
-            sum_t, guess, guess_sq = newton[t]
+        def step_y(t):
             near_one = ring.tile([P, S], F32, name="near_one")
-            nc.vector.scalar_tensor_tensor(near_one[:], sum_t[:], 0.05, guess_sq[:], ALU.add, ALU.mult)
-            near.append(near_one)
+            nc.vector.scalar_tensor_tensor(near_one[:], st[t]["sq_sum"][:], 0.05, st[t]["guess_sq"][:], ALU.add, ALU.mult)
+            st[t]["near_one"] = near_one
 
-        def polish_b(t):
-            guess = newton[t][1]
+        def step_r(t):
             inv_t = ring.tile([P, S], F32, name="inv_t")
-            nc.vector.scalar_tensor_tensor(inv_t[:], near[t][:], -3.0, guess[:], ALU.add, ALU.mult)
-            inv = psum.tile([P, S], F32, name="inv", tag="inv", bufs=4)
-            for j in range(PACK):
-                cols = slice(P * j, P * (j + 1))
-                nc.tensor.transpose(inv[:, cols], inv_t[:, cols], ident[:])
-            inv_norm.append(inv)
+            nc.vector.scalar_tensor_tensor(inv_t[:], st[t]["near_one"][:], -3.0, st[t]["guess"][:], ALU.add, ALU.mult)
+            inv = psum.tile([P, S], F32, name="inv", tag="inv")
+            turn(inv, [inv_t[:]])
+            st[t]["inv_t"] = inv_t
+            st[t]["inv"] = inv
 
-        def gradient_sum(t):
-            nc.vector.tensor_tensor(gsum[t][:], grad[t][:, 0, :], grad[t][:, 1, :], ALU.add)
+        def step_s(t):
+            v_sum_t = ring.tile([P, S], F32, name="v_sum_t")
+            nc.vector.scalar_tensor_tensor(v_sum_t[:], st[t]["g_sum"][:], -0.5, st[t]["inv_t"][:], ALU.mult, ALU.mult)
+            v_sum = psum.tile([P, S], F32, name="v_sum", tag="mm")
+            turn(v_sum, [v_sum_t[:]])
+            st[t]["v_sum"] = v_sum
 
-        fetched = []
+        def step_copy(t):
+            window = ring.tile([P, S], F32, name="window")
+            nc.scalar.activation(window[:], st[t]["v_sum"][:], ACT.Copy, scale=unit_sb[:, t : t + 1])
+            st[t]["window"] = window
 
-        def normalise(t):
-            nc.vector.scalar_tensor_tensor(vsum[t][:], gsum[t][:], -0.5, inv_norm[t][:], ALU.mult, ALU.mult)
-            nc.vector.scalar_tensor_tensor(
-                term_vx[:, t, :], grad[t][:, 0, :], half_unit[:, t : t + 1], inv_norm[t][:], ALU.mult, ALU.mult
-            )
+        def step_fetch(t):
+            window = st[t]["window"]
             got = ring.tile([P, S], F32, name="got")
             for a in range(2):
-                nc.scalar.activation(
-                    got[:, HALF * a : HALF * (a + 1)], vsum[t][:].indirect(h3_sb[:, 16 * a : 16 * (a + 1)]), ACT.Copy
-                )
-            fetched.append(got)
+                nc.scalar.activation(got[:, halves[a]], window[:].indirect(h3_sb[:, list_halves[a]]), ACT.Copy)
+            st[t]["got"] = got
 
-        def divergence(t):
+        def step_w(t):
+            nc.vector.scalar_tensor_tensor(
+                term_vx[:, t, :], st[t]["inv"][:], quarter_unit[:, t : t + 1], grad[t][:, 0, :], ALU.mult, ALU.mult
+            )
+
+        def step_d(t):
             div = ring.tile([P, S], F32, name="div")
-            nc.vector.tensor_tensor(div[:], vsum[t][:], fetched[t][:], ALU.subtract)
-            return div
+            nc.vector.tensor_tensor(div[:], st[t]["window"][:], st[t]["got"][:], ALU.subtract)
+            st[t]["div"] = div
 
-        def weigh(t, div):
-            nc.vector.scalar_tensor_tensor(term_div[:, t, :], div[:], unit_sb[:, t : t + 1], heat[t][:], ALU.mult, ALU.mult)
+        def step_t(t):
+            nc.vector.tensor_tensor(term_div[:, t, :], st[t]["div"][:], heat[t][:], ALU.mult)
 
-        gradients(0)
-        norm(0)
-        gradients(1)
-        norm(1)
-        gradient_sum(0)
-        gradients(2)
-        gradient_sum(1)
-        polish_a(0)
-        gradient_sum(2)
-        polish_b(0)
-        norm(2)
-        gradients(3)
-        polish_a(1)
-        gradient_sum(3)
-        polish_b(1)
-        norm(3)
-        normalise(0)
-        normalise(1)
-        polish_a(2)
-        div = divergence(0)
-        polish_b(2)
-        weigh(0, div)
-        polish_a(3)
-        div = divergence(1)
-        polish_b(3)
-        weigh(1, div)
-        normalise(2)
-        normalise(3)
-        div2 = divergence(2)
-        weigh(2, div2)
-        div3 = divergence(3)
-        weigh(3, div3)
+        gradient(0, 0)
+        gradient(0, 1)
+        gradient(1, 0)
+        gradient(1, 1)
+        square(0)
+        gradient(2, 0)
+        gradient(2, 1)
+        gradient(3, 0)
+        guess_root(0)
+        square(1)
+        square(2)
+        step_y(0)
+        gradient(3, 1)
+        guess_root(1)
+        step_r(0)
+        guess_root(2)
+        step_y(1)
+        square(3)
+        step_s(0)
+        step_r(1)
+        step_copy(0)
+        step_w(0)
+        guess_root(3)
+        step_y(2)
+        step_fetch(0)
+        step_s(1)
+        step_r(2)
+        step_copy(1)
+        step_fetch(1)
+        step_w(1)
+        step_y(3)
+        step_s(2)
+        step_r(3)
+        step_copy(2)
+        step_fetch(2)
+        step_w(2)
+        step_s(3)
+        step_copy(3)
+        step_fetch(3)
+        step_w(3)
+        step_d(0)
+        step_d(1)
+        step_t(0)
+        step_d(2)
+        step_t(1)
+        step_d(3)
+        step_t(2)
+        step_t(3)
+
 
         out_v = out.rearrange("(m p) n -> p m n", p=P)
-        for c0, width in CHUNKS:
+
+        def add_terms(c0, width):
             cols = slice(c0, c0 + width)
             hid = keep.tile([P, width, PACK], BF16, name=f"hid{c0}", align_bytes=64)
             nc.vector.tensor_tensor(
@@ -215,10 +259,14 @@ def tile_picked_yheatg_mul_p_kernel(tc, x_words, x_scales, w1_words, w1_scales, 
                 term_vx[:, :, cols].rearrange("p t (c i) -> p c t i", i=4),
                 ALU.add,
             )
+            return hid
+
+        def finish(c0, width, hid, bank_tag):
+            cols = slice(c0, c0 + width)
             codes = keep.tile([P, width], U32, name=f"codes{c0}", align_bytes=64)
             scales = keep.tile([P, width], U8, name=f"scales{c0}", align_bytes=64)
             nc.vector.quantize_mx(out=codes[:].bitcast(FP8X4), scales=scales[:], in_=hid[:].rearrange("p n t -> p (n t)"))
-            acc = psum.tile([P, 2, width], F32, name="acc", tag="mm")
+            acc = psum.tile([P, 2, width], F32, name="acc", tag=bank_tag)
             for m in range(2):
                 nc.tensor.matmul_mx(
                     out=acc[:, m, :],
@@ -232,3 +280,9 @@ def tile_picked_yheatg_mul_p_kernel(tc, x_words, x_scales, w1_words, w1_scales, 
             res = keep.tile([P, 2, width], F32, name=f"res{c0}")
             nc.scalar.copy(res[:], acc[:])
             nc.sync.dma_start(out=out_v[:, :, cols], in_=res[:])
+
+        first = add_terms(*CHUNKS[0])
+        second = add_terms(*CHUNKS[1])
+        finish(*CHUNKS[0], first, "sq_sum")
+        finish(*CHUNKS[1], second, "g_sum")
+        finish(*CHUNKS[2], add_terms(*CHUNKS[2]), "inv")

@@ -40,13 +40,13 @@ def tile_picked_yheatg_mul_p_kernel(tc, x_words, x_scales, w1_words, w1_scales, 
     with ExitStack() as ctx:
         keep = ctx.enter_context(tc.tile_pool(name="keep", bufs=1))
         ring = ctx.enter_context(tc.tile_pool(name="ring", bufs=PACK))
-        psum = ctx.enter_context(tc.psum_pool(name="psum", bufs=2))
+        psum = ctx.enter_context(tc.psum_pool(name="psum", bufs=1))
 
         offs_sb = keep.tile([P, S // 16], U16, name="offs_sb")
         h1_sb = keep.tile([P, S // 16], U16, name="h1_sb")
         h2_sb = keep.tile([P, S // 16], U16, name="h2_sb")
         h3_sb = keep.tile([P, S // 16], U16, name="h3_sb")
-        xw = keep.tile([P, T], U32, name="xw", align_bytes=64)
+        xw = keep.tile([P, T], U32, name="xw", tag="x_bytes", align_bytes=64)
         xs = keep.tile([P, T], U8, name="xs", align_bytes=64)
         w1w = keep.tile([P, 2 * H], U8, name="w1w", align_bytes=64)
         w1s = keep.tile([P, H], U8, name="w1s", tag="w1_bytes", align_bytes=64)
@@ -77,20 +77,18 @@ def tile_picked_yheatg_mul_p_kernel(tc, x_words, x_scales, w1_words, w1_scales, 
         w1s_dealt = keep.tile([P, PACK, P], U8, name="w1s_dealt", align_bytes=64)
         w1w_by_tile = w1w[:].rearrange("p (m t b) -> p t m b", t=PACK, b=2)
 
-        def deal_scales(tiles):
-            nc.vector.tensor_copy(out=w1s_dealt[:, tiles, :], in_=w1s[:].rearrange("p (m t) -> p t m", t=PACK)[:, tiles])
-
         xg_s = keep.tile([P, S], U8, name="xg_s", align_bytes=64)
-        xg_w = keep.tile([P, S], U32, name="xg_w", align_bytes=64)
+        xg_first = keep.tile([P, HALF], U32, name="xg_first", align_bytes=64)
         halves = [slice(0, HALF), slice(HALF, S)]
         list_halves = [slice(0, HALF // 16), slice(HALF // 16, S // 16)]
         nc.vector.tensor_copy(xg_s[:], xs[:].indirect(offs_sb[:]))
         nc.vector.tensor_copy(out=w1w_first[:].rearrange("p (m b) -> p m b", b=2), in_=w1w_by_tile[:, 0])
-        nc.vector.tensor_copy(xg_w[:, halves[0]], xw[:].indirect(offs_sb[:, list_halves[0]]))
-        deal_scales(slice(0, 1))
-        nc.vector.tensor_copy(xg_w[:, halves[1]], xw[:].indirect(offs_sb[:, list_halves[1]]))
-        deal_scales(slice(1, PACK))
-        w1w_rest = keep.tile([P, PACK - 1, 2 * P], U8, name="w1w_rest", tag="w1_bytes", align_bytes=64)
+        nc.vector.tensor_copy(xg_first[:], xw[:].indirect(offs_sb[:, list_halves[0]]))
+        nc.vector.tensor_copy(out=w1s_dealt[:], in_=w1s[:].rearrange("p (m t) -> p t m", t=PACK))
+        xg_second = keep.tile([P, HALF], U32, name="xg_second", tag="w1_bytes", align_bytes=64)
+        nc.vector.tensor_copy(xg_second[:], xw[:].indirect(offs_sb[:, list_halves[1]]))
+        xg_w = [xg_first, xg_second]
+        w1w_rest = keep.tile([P, PACK - 1, 2 * P], U8, name="w1w_rest", tag="x_bytes", align_bytes=64)
         nc.vector.tensor_copy(out=w1w_rest[:].rearrange("p t (m b) -> p t m b", b=2), in_=w1w_by_tile[:, 1:])
         w1_tiles = [w1w_first[:]] + [w1w_rest[:, t, :] for t in range(PACK - 1)]
 
@@ -100,26 +98,36 @@ def tile_picked_yheatg_mul_p_kernel(tc, x_words, x_scales, w1_words, w1_scales, 
         term_div = keep.tile([P, PACK, S], F32, name="term_div")
         term_vx = keep.tile([P, PACK, S], F32, name="term_vx")
 
-        for t in range(PACK):
-            for cols in halves if t == 0 else [slice(0, S)]:
-                width = cols.stop - cols.start
-                uu = psum.tile([P, width], F32, name="uu", tag="mm")
-                nc.tensor.matmul_mx(
-                    out=uu[:],
-                    lhsT=w1_tiles[t].bitcast(FP4X4),
-                    lhsT_scale=w1s_dealt[:, t, :],
-                    rhs=xg_w[:, cols].bitcast(FP8X4),
-                    rhs_scale=xg_s[:, cols],
-                    start=True,
-                    stop=True,
-                )
-                tanh_cols = slice(S + cols.start, S + cols.stop)
-                nc.scalar.activation(heat_win[t][:, tanh_cols], uu[:], ACT.Tanh)
-                nc.scalar.activation(heat_win[t][:, cols], heat_win[t][:, tanh_cols], ACT.Exp, scale=0.8)
-                if t < 2:
-                    nc.vector.tensor_copy(heat[t][:, cols], heat_win[t][:, cols])
-                else:
-                    nc.sync.dma_start(out=heat[t][:], in_=heat_win[t][:, :S])
+        def first_product(bank, t, a):
+            nc.tensor.matmul_mx(
+                out=bank,
+                lhsT=w1_tiles[t].bitcast(FP4X4),
+                lhsT_scale=w1s_dealt[:, t, :],
+                rhs=xg_w[a][:].bitcast(FP8X4),
+                rhs_scale=xg_s[:, halves[a]],
+                start=True,
+                stop=True,
+            )
+
+        def make_heat(t, cols, bank):
+            tanh_cols = slice(S + cols.start, S + cols.stop)
+            nc.scalar.activation(heat_win[t][:, tanh_cols], bank, ACT.Tanh)
+            nc.scalar.activation(heat_win[t][:, cols], heat_win[t][:, tanh_cols], ACT.Exp, scale=0.8)
+
+        for a in range(2):
+            uu = psum.tile([P, HALF], F32, name="uu", tag=("norm0", "spare")[a])
+            first_product(uu[:], 0, a)
+            make_heat(0, halves[a], uu[:])
+            nc.vector.tensor_copy(heat[0][:, halves[a]], heat_win[0][:, halves[a]])
+        for t in range(1, PACK):
+            uu = psum.tile([P, S], F32, name="uu", tag=f"norm{t}")
+            for a in range(2):
+                first_product(uu[:, halves[a]], t, a)
+            make_heat(t, slice(0, S), uu[:])
+            if t == 1:
+                nc.vector.tensor_copy(heat[t][:], heat_win[t][:, :S])
+            else:
+                nc.sync.dma_start(out=heat[t][:], in_=heat_win[t][:, :S])
 
         def turn(bank, parts):
             for j in range(PACK):
@@ -138,7 +146,7 @@ def tile_picked_yheatg_mul_p_kernel(tc, x_words, x_scales, w1_words, w1_scales, 
         def square(t):
             squares = keep.tile([P, 2, S], F32, name="squares", tag=f"squares{max(t, 1)}")
             nc.scalar.activation(squares[:], grad[t][:], ACT.Square)
-            sq_sum = psum.tile([P, S], F32, name="sq_sum", tag="sq_sum")
+            sq_sum = psum.tile([P, S], F32, name="sq_sum", tag=f"norm{t}")
             turn(sq_sum, [squares[:, 0, :], squares[:, 1, :]])
             st[t]["sq_sum"] = sq_sum
 
@@ -149,7 +157,9 @@ def tile_picked_yheatg_mul_p_kernel(tc, x_words, x_scales, w1_words, w1_scales, 
             nc.scalar.activation(guess_sq[:], guess[:], ACT.Square)
             st[t]["guess"] = guess
             st[t]["guess_sq"] = guess_sq
-            g_sum = psum.tile([P, S], F32, name="g_sum", tag="g_sum")
+
+        def step_p(t):
+            g_sum = psum.tile([P, S], F32, name="g_sum", tag=f"sum{t % 3}")
             turn(g_sum, [grad[t][:, 0, :], grad[t][:, 1, :]])
             st[t]["g_sum"] = g_sum
 
@@ -161,28 +171,27 @@ def tile_picked_yheatg_mul_p_kernel(tc, x_words, x_scales, w1_words, w1_scales, 
         def step_r(t):
             inv_t = ring.tile([P, S], F32, name="inv_t")
             nc.vector.scalar_tensor_tensor(inv_t[:], st[t]["near_one"][:], -3.0, st[t]["guess"][:], ALU.add, ALU.mult)
-            inv = psum.tile([P, S], F32, name="inv", tag="inv")
+            inv = psum.tile([P, S], F32, name="inv", tag=f"norm{t}")
             turn(inv, [inv_t[:]])
             st[t]["inv_t"] = inv_t
             st[t]["inv"] = inv
 
         def step_s(t):
-            v_sum_t = ring.tile([P, S], F32, name="v_sum_t")
-            nc.vector.scalar_tensor_tensor(v_sum_t[:], st[t]["g_sum"][:], -0.5, st[t]["inv_t"][:], ALU.mult, ALU.mult)
-            v_sum = psum.tile([P, S], F32, name="v_sum", tag="mm")
-            turn(v_sum, [v_sum_t[:]])
+            window = ring.tile([P, 2 * S], F32, name="window")
+            st[t]["window"] = window
+            v_sum_t = window[:, S:]
+            nc.vector.scalar_tensor_tensor(v_sum_t, st[t]["g_sum"][:], -0.5, st[t]["inv_t"][:], ALU.mult, ALU.mult)
+            v_sum = psum.tile([P, S], F32, name="v_sum", tag=f"sum{t % 3}")
+            turn(v_sum, [v_sum_t])
             st[t]["v_sum"] = v_sum
 
         def step_copy(t):
-            window = ring.tile([P, S], F32, name="window")
-            nc.scalar.activation(window[:], st[t]["v_sum"][:], ACT.Copy, scale=unit_sb[:, t : t + 1])
-            st[t]["window"] = window
+            nc.scalar.activation(st[t]["window"][:, :S], st[t]["v_sum"][:], ACT.Copy, scale=unit_sb[:, t : t + 1])
 
         def step_fetch(t):
             window = st[t]["window"]
             got = ring.tile([P, S], F32, name="got")
-            for a in range(2):
-                nc.scalar.activation(got[:, halves[a]], window[:].indirect(h3_sb[:, list_halves[a]]), ACT.Copy)
+            nc.scalar.activation(got[:], window[:].indirect(h3_sb[:]), ACT.Copy)
             st[t]["got"] = got
 
         def step_w(t):
@@ -192,7 +201,7 @@ def tile_picked_yheatg_mul_p_kernel(tc, x_words, x_scales, w1_words, w1_scales, 
 
         def step_d(t):
             div = ring.tile([P, S], F32, name="div")
-            nc.vector.tensor_tensor(div[:], st[t]["window"][:], st[t]["got"][:], ALU.subtract)
+            nc.vector.tensor_tensor(div[:], st[t]["window"][:, :S], st[t]["got"][:], ALU.subtract)
             st[t]["div"] = div
 
         def step_t(t):
@@ -203,12 +212,15 @@ def tile_picked_yheatg_mul_p_kernel(tc, x_words, x_scales, w1_words, w1_scales, 
         gradient(1, 0)
         gradient(1, 1)
         square(0)
+        step_p(0)
         gradient(2, 0)
         gradient(2, 1)
         gradient(3, 0)
         guess_root(0)
         square(1)
+        step_p(1)
         square(2)
+        step_p(2)
         step_y(0)
         gradient(3, 1)
         guess_root(1)
@@ -221,6 +233,7 @@ def tile_picked_yheatg_mul_p_kernel(tc, x_words, x_scales, w1_words, w1_scales, 
         step_copy(0)
         step_w(0)
         guess_root(3)
+        step_p(3)
         step_y(2)
         step_fetch(0)
         step_s(1)
@@ -254,35 +267,54 @@ def tile_picked_yheatg_mul_p_kernel(tc, x_words, x_scales, w1_words, w1_scales, 
             cols = slice(c0, c0 + width)
             hid = keep.tile([P, width, PACK], BF16, name=f"hid{c0}", align_bytes=64)
             nc.vector.tensor_tensor(
-                hid[:].rearrange("p (c i) t -> p c t i", i=4),
-                term_div[:, :, cols].rearrange("p t (c i) -> p c t i", i=4),
-                term_vx[:, :, cols].rearrange("p t (c i) -> p c t i", i=4),
+                hid[:].rearrange("p (c i) t -> p c t i", i=2),
+                term_div[:, :, cols].rearrange("p t (c i) -> p c t i", i=2),
+                term_vx[:, :, cols].rearrange("p t (c i) -> p c t i", i=2),
                 ALU.add,
             )
             return hid
 
-        def finish(c0, width, hid, bank_tag):
-            cols = slice(c0, c0 + width)
+        def quantise(c0, width, hid):
             codes = keep.tile([P, width], U32, name=f"codes{c0}", align_bytes=64)
             scales = keep.tile([P, width], U8, name=f"scales{c0}", align_bytes=64)
             nc.vector.quantize_mx(out=codes[:].bitcast(FP8X4), scales=scales[:], in_=hid[:].rearrange("p n t -> p (n t)"))
+            return codes, scales
+
+        def product(acc, m, codes, scales):
+            nc.tensor.matmul_mx(
+                out=acc,
+                lhsT=w2w[:, 2 * P * m : 2 * P * (m + 1)].bitcast(FP4X4),
+                lhsT_scale=w2s[:, P * m : P * (m + 1)],
+                rhs=codes[:].bitcast(FP8X4),
+                rhs_scale=scales[:],
+                start=True,
+                stop=True,
+            )
+
+        def finish(c0, width, hid, bank_tag):
+            codes, scales = quantise(c0, width, hid)
             acc = psum.tile([P, 2, width], F32, name="acc", tag=bank_tag)
             for m in range(2):
-                nc.tensor.matmul_mx(
-                    out=acc[:, m, :],
-                    lhsT=w2w[:, 2 * P * m : 2 * P * (m + 1)].bitcast(FP4X4),
-                    lhsT_scale=w2s[:, P * m : P * (m + 1)],
-                    rhs=codes[:].bitcast(FP8X4),
-                    rhs_scale=scales[:],
-                    start=True,
-                    stop=True,
-                )
+                product(acc[:, m, :], m, codes, scales)
             res = keep.tile([P, 2, width], F32, name=f"res{c0}")
             nc.scalar.copy(res[:], acc[:])
-            nc.sync.dma_start(out=out_v[:, :, cols], in_=res[:])
+            nc.sync.dma_start(out=out_v[:, :, c0 : c0 + width], in_=res[:])
+
+        def finish_last(c0, width, hid):
+            codes, scales = quantise(c0, width, hid)
+            for m in range(2):
+                acc = psum.tile([P, width], F32, name="acc", tag=f"norm{2 + m}")
+                product(acc[:], m, codes, scales)
+                res = keep.tile([P, width], F32, name=f"res_last{m}")
+                if m == 0:
+                    nc.scalar.copy(res[:], acc[:])
+                    nc.scalar.dma_start(out=out_v[:, m, c0 : c0 + width], in_=res[:])
+                else:
+                    nc.vector.tensor_copy(res[:], acc[:])
+                    nc.sync.dma_start(out=out_v[:, m, c0 : c0 + width], in_=res[:])
 
         first = add_terms(*CHUNKS[0])
         second = add_terms(*CHUNKS[1])
-        finish(*CHUNKS[0], first, "sq_sum")
-        finish(*CHUNKS[1], second, "g_sum")
-        finish(*CHUNKS[2], add_terms(*CHUNKS[2]), "inv")
+        finish(*CHUNKS[0], first, "norm0")
+        finish(*CHUNKS[1], second, "norm1")
+        finish_last(*CHUNKS[2], add_terms(*CHUNKS[2]))

@@ -72,6 +72,8 @@ def tile_picked_yheatg_mul_p_kernel(tc, x_words, x_scales, w1_words, w1_scales, 
 
         quarter_unit = keep.tile([P, PACK], F32, name="quarter_unit")
         nc.gpsimd.tensor_scalar(quarter_unit[:], unit_sb[:], 0.25, 0.0, ALU.mult, ALU.add)
+        minus_half_unit = keep.tile([P, PACK], F32, name="minus_half_unit")
+        nc.gpsimd.tensor_scalar(minus_half_unit[:], unit_sb[:], -0.5, 0.0, ALU.mult, ALU.add)
 
         w1w_first = keep.tile([P, 2 * P], U8, name="w1w_first", align_bytes=64)
         w1s_dealt = keep.tile([P, PACK, P], U8, name="w1s_dealt", align_bytes=64)
@@ -92,7 +94,7 @@ def tile_picked_yheatg_mul_p_kernel(tc, x_words, x_scales, w1_words, w1_scales, 
         nc.vector.tensor_copy(out=w1w_rest[:].rearrange("p t (m b) -> p t m b", b=2), in_=w1w_by_tile[:, 1:])
         w1_tiles = [w1w_first[:]] + [w1w_rest[:, t, :] for t in range(PACK - 1)]
 
-        heat_win = [keep.tile([P, 2 * S], F32, name=f"heat_win{t}") for t in range(PACK)]
+        heat_win = [keep.tile([P, 2 * S], F32, name=f"heat_win{t}", tag=f"heat_win{t}") for t in range(PACK)]
         heat = [keep.tile([P, S], F32, name=f"heat{t}") for t in range(PACK)]
         grad = [keep.tile([P, 2, S], F32, name=f"grad{t}") for t in range(PACK)]
         term_div = keep.tile([P, PACK, S], F32, name="term_div")
@@ -109,25 +111,29 @@ def tile_picked_yheatg_mul_p_kernel(tc, x_words, x_scales, w1_words, w1_scales, 
                 stop=True,
             )
 
-        def make_heat(t, cols, bank):
-            tanh_cols = slice(S + cols.start, S + cols.stop)
-            nc.scalar.activation(heat_win[t][:, tanh_cols], bank, ACT.Tanh)
-            nc.scalar.activation(heat_win[t][:, cols], heat_win[t][:, tanh_cols], ACT.Exp, scale=0.8)
+        def squash(t, cols, bank):
+            nc.scalar.activation(heat_win[t][:, S + cols.start : S + cols.stop], bank, ACT.Tanh)
+
+        def make_heat(t, cols):
+            nc.scalar.activation(heat_win[t][:, cols], heat_win[t][:, S + cols.start : S + cols.stop], ACT.Exp, scale=0.8)
+            if t < 2:
+                nc.vector.tensor_copy(heat[t][:, cols], heat_win[t][:, cols])
+            else:
+                nc.sync.dma_start(out=heat[t][:], in_=heat_win[t][:, :S])
 
         for a in range(2):
             uu = psum.tile([P, HALF], F32, name="uu", tag=("norm0", "spare")[a])
             first_product(uu[:], 0, a)
-            make_heat(0, halves[a], uu[:])
-            nc.vector.tensor_copy(heat[0][:, halves[a]], heat_win[0][:, halves[a]])
+            squash(0, halves[a], uu[:])
+            make_heat(0, halves[a])
         for t in range(1, PACK):
             uu = psum.tile([P, S], F32, name="uu", tag=f"norm{t}")
             for a in range(2):
                 first_product(uu[:, halves[a]], t, a)
-            make_heat(t, slice(0, S), uu[:])
-            if t == 1:
-                nc.vector.tensor_copy(heat[t][:], heat_win[t][:, :S])
-            else:
-                nc.sync.dma_start(out=heat[t][:], in_=heat_win[t][:, :S])
+            squash(t, slice(0, S), uu[:])
+            if t > 1:
+                make_heat(t - 1, slice(0, S))
+        make_heat(PACK - 1, slice(0, S))
 
         def turn(bank, parts):
             for j in range(PACK):
@@ -153,18 +159,15 @@ def tile_picked_yheatg_mul_p_kernel(tc, x_words, x_scales, w1_words, w1_scales, 
         def guess_root(t):
             guess = ring.tile([P, S], F32, name="guess")
             nc.scalar.activation(guess[:], st[t]["sq_sum"][:], ACT.Abs_reciprocal_sqrt, bias=0.05)
-            guess_sq = ring.tile([P, S], F32, name="guess_sq")
-            nc.scalar.activation(guess_sq[:], guess[:], ACT.Square)
             st[t]["guess"] = guess
+
+        def square_guess(t):
+            guess_sq = ring.tile([P, S], F32, name="guess_sq")
+            nc.scalar.activation(guess_sq[:], st[t]["guess"][:], ACT.Square)
             st[t]["guess_sq"] = guess_sq
 
-        def step_p(t):
-            g_sum = psum.tile([P, S], F32, name="g_sum", tag=f"sum{t % 3}")
-            turn(g_sum, [grad[t][:, 0, :], grad[t][:, 1, :]])
-            st[t]["g_sum"] = g_sum
-
         def step_y(t):
-            near_one = ring.tile([P, S], F32, name="near_one")
+            near_one = keep.tile([P, S], F32, name="near_one", tag=f"near_one{t}")
             nc.vector.scalar_tensor_tensor(near_one[:], st[t]["sq_sum"][:], 0.05, st[t]["guess_sq"][:], ALU.add, ALU.mult)
             st[t]["near_one"] = near_one
 
@@ -173,35 +176,34 @@ def tile_picked_yheatg_mul_p_kernel(tc, x_words, x_scales, w1_words, w1_scales, 
             nc.vector.scalar_tensor_tensor(inv_t[:], st[t]["near_one"][:], -3.0, st[t]["guess"][:], ALU.add, ALU.mult)
             inv = psum.tile([P, S], F32, name="inv", tag=f"norm{t}")
             turn(inv, [inv_t[:]])
-            st[t]["inv_t"] = inv_t
             st[t]["inv"] = inv
 
-        def step_s(t):
-            window = ring.tile([P, 2 * S], F32, name="window")
-            st[t]["window"] = window
-            v_sum_t = window[:, S:]
-            nc.vector.scalar_tensor_tensor(v_sum_t, st[t]["g_sum"][:], -0.5, st[t]["inv_t"][:], ALU.mult, ALU.mult)
-            v_sum = psum.tile([P, S], F32, name="v_sum", tag=f"sum{t % 3}")
-            turn(v_sum, [v_sum_t])
-            st[t]["v_sum"] = v_sum
-
-        def step_copy(t):
-            nc.scalar.activation(st[t]["window"][:, :S], st[t]["v_sum"][:], ACT.Copy, scale=unit_sb[:, t : t + 1])
-
-        def step_fetch(t):
-            window = st[t]["window"]
-            got = ring.tile([P, S], F32, name="got")
-            nc.scalar.activation(got[:], window[:].indirect(h3_sb[:]), ACT.Copy)
-            st[t]["got"] = got
+        def step_p(t):
+            g_sum = keep.tile([P, S], F32, name="g_sum", tag=f"near_one{t}" if t else f"heat_win{PACK - 1}")
+            nc.gpsimd.tensor_tensor(g_sum[:], grad[t][:, 0, :], grad[t][:, 1, :], ALU.add)
+            st[t]["g_sum"] = g_sum
 
         def step_w(t):
             nc.vector.scalar_tensor_tensor(
                 term_vx[:, t, :], st[t]["inv"][:], quarter_unit[:, t : t + 1], grad[t][:, 0, :], ALU.mult, ALU.mult
             )
 
+        def step_s(t):
+            window = ring.tile([P, S], F32, name="window")
+            nc.vector.scalar_tensor_tensor(
+                window[:], st[t]["inv"][:], minus_half_unit[:, t : t + 1], st[t]["g_sum"][:], ALU.mult, ALU.mult
+            )
+            st[t]["window"] = window
+
+        def step_fetch(t):
+            got = ring.tile([P, S], F32, name="got")
+            for a in range(2):
+                nc.scalar.activation(got[:, halves[a]], st[t]["window"][:].indirect(h3_sb[:, list_halves[a]]), ACT.Copy)
+            st[t]["got"] = got
+
         def step_d(t):
             div = ring.tile([P, S], F32, name="div")
-            nc.vector.tensor_tensor(div[:], st[t]["window"][:, :S], st[t]["got"][:], ALU.subtract)
+            nc.vector.tensor_tensor(div[:], st[t]["window"][:], st[t]["got"][:], ALU.subtract)
             st[t]["div"] = div
 
         def step_t(t):
@@ -212,45 +214,45 @@ def tile_picked_yheatg_mul_p_kernel(tc, x_words, x_scales, w1_words, w1_scales, 
         gradient(1, 0)
         gradient(1, 1)
         square(0)
-        step_p(0)
         gradient(2, 0)
         gradient(2, 1)
         gradient(3, 0)
+        gradient(3, 1)
         guess_root(0)
         square(1)
-        step_p(1)
+        square_guess(0)
         square(2)
-        step_p(2)
-        step_y(0)
-        gradient(3, 1)
         guess_root(1)
-        step_r(0)
-        guess_root(2)
+        square_guess(1)
+        step_p(0)
+        step_y(0)
         step_y(1)
+        guess_root(2)
         square(3)
-        step_s(0)
+        square_guess(2)
+        step_r(0)
         step_r(1)
-        step_copy(0)
+        step_p(1)
+        step_y(2)
+        step_s(0)
         step_w(0)
         guess_root(3)
-        step_p(3)
-        step_y(2)
+        square_guess(3)
         step_fetch(0)
-        step_s(1)
         step_r(2)
-        step_copy(1)
-        step_fetch(1)
-        step_w(1)
+        step_p(2)
         step_y(3)
-        step_s(2)
+        step_s(1)
+        step_w(1)
+        step_fetch(1)
         step_r(3)
-        step_copy(2)
-        step_fetch(2)
+        step_p(3)
+        step_s(2)
         step_w(2)
-        step_s(3)
-        step_copy(3)
-        step_fetch(3)
+        step_fetch(2)
         step_w(3)
+        step_s(3)
+        step_fetch(3)
         step_d(0)
         step_d(1)
         step_t(0)

@@ -19,33 +19,42 @@ ALU = mybir.AluOpType
 
 P = 128
 PACK = 4
+LAST = PACK - 1
+QUADRANTS = 4
+GROUP = 16
 HALF = S // 2
-CHUNKS = ((0, 256), (256, 128), (384, 128))
+HALVES = (slice(0, HALF), slice(HALF, S))
+LIST_HALVES = (slice(0, HALF // GROUP), slice(HALF // GROUP, S // GROUP))
+ALL = slice(0, S)
+WIDE, NARROW, FINAL = (0, 256), (256, 128), (384, 128)
 
 
-def load_scale_rows(queue, plane, rows, quadrants):
-    for q in quadrants:
-        queue.dma_start(out=plane[32 * q : 32 * q + 4, :].bitcast(I32), in_=rows[4 * q : 4 * q + 4, :].bitcast(I32))
+def load_scale_rows(nc, plane, rows):
+    for q in range(QUADRANTS):
+        nc.sync.dma_start(out=plane[32 * q : 32 * q + 4, :].bitcast(I32), in_=rows[4 * q : 4 * q + 4, :].bitcast(I32))
 
 
-def load_scale_rows_repeated(queue, plane, rows, quadrants):
-    width = rows.shape[1] // 4
-    for q in quadrants:
-        four = rows[4 * q : 4 * q + 4, :].bitcast(I32)
-        queue.dma_start(out=plane[32 * q : 32 * q + 32, :].bitcast(I32), in_=four.unsqueeze(0).to_broadcast([8, 4, width]))
+def load_scale_rows_for_copy(nc, plane, rows):
+    words = rows.shape[1] // 4
+    for q in range(QUADRANTS):
+        four_rows = rows[4 * q : 4 * q + 4, :].bitcast(I32)
+        nc.sync.dma_start(
+            out=plane[32 * q : 32 * q + 32, :].bitcast(I32), in_=four_rows.unsqueeze(0).to_broadcast([8, 4, words])
+        )
 
 
-def tile_picked_yheatg_mul_p_kernel(tc, x_words, x_scales, w1_words, w1_scales, unit, w2_words, w2_scales, offs, h1, h2, h3, out):
+def tile_picked_yheatg_mul_p_kernel(
+    tc, x_words, x_scales, w1_words, w1_scales, unit, w2_words, w2_scales, offs, h1, h2, h3, out
+):
     nc = tc.nc
     with ExitStack() as ctx:
         keep = ctx.enter_context(tc.tile_pool(name="keep", bufs=1))
-        ring = ctx.enter_context(tc.tile_pool(name="ring", bufs=PACK))
         psum = ctx.enter_context(tc.psum_pool(name="psum", bufs=1))
 
-        offs_sb = keep.tile([P, S // 16], U16, name="offs_sb")
-        h1_sb = keep.tile([P, S // 16], U16, name="h1_sb")
-        h2_sb = keep.tile([P, S // 16], U16, name="h2_sb")
-        h3_sb = keep.tile([P, S // 16], U16, name="h3_sb")
+        offs_sb = keep.tile([P, S // GROUP], U16, name="offs_sb")
+        h1_sb = keep.tile([P, S // GROUP], U16, name="h1_sb")
+        h2_sb = keep.tile([P, S // GROUP], U16, name="h2_sb")
+        h3_sb = keep.tile([P, S // GROUP], U16, name="h3_sb")
         xw = keep.tile([P, T], U32, name="xw", tag="x_bytes", align_bytes=64)
         xs = keep.tile([P, T], U8, name="xs", align_bytes=64)
         w1w = keep.tile([P, 2 * H], U8, name="w1w", align_bytes=64)
@@ -56,18 +65,17 @@ def tile_picked_yheatg_mul_p_kernel(tc, x_words, x_scales, w1_words, w1_scales, 
         ident = keep.tile([P, P], F32, name="ident")
 
         nc.gpsimd.memset(w2s[:].bitcast(I32), 0)
-
         nc.sync.dma_start(offs_sb[:], offs)
-        load_scale_rows_repeated(nc.sync, xs, x_scales[0], range(4))
+        load_scale_rows_for_copy(nc, xs, x_scales[0])
         nc.sync.dma_start(out=w1w[:].bitcast(I32), in_=w1_words[0].bitcast(I32))
         nc.sync.dma_start(out=xw[:].bitcast(I32), in_=x_words[0].rearrange("p n t -> p (n t)").bitcast(I32))
-        load_scale_rows_repeated(nc.sync, w1s, w1_scales[0], range(4))
+        load_scale_rows_for_copy(nc, w1s, w1_scales[0])
         nc.sync.dma_start(h1_sb[:], h1)
         nc.sync.dma_start(h2_sb[:], h2)
         nc.sync.dma_start(out=unit_sb[:], in_=unit.rearrange("(p t) o -> p (t o)", t=PACK))
         nc.sync.dma_start(h3_sb[:], h3)
         nc.sync.dma_start(out=w2w[:].bitcast(I32), in_=w2_words[0].bitcast(I32))
-        load_scale_rows(nc.sync, w2s, w2_scales[0], range(4))
+        load_scale_rows(nc, w2s, w2_scales[0])
         make_identity(nc, ident[:])
 
         quarter_unit = keep.tile([P, PACK], F32, name="quarter_unit")
@@ -75,199 +83,171 @@ def tile_picked_yheatg_mul_p_kernel(tc, x_words, x_scales, w1_words, w1_scales, 
         minus_half_unit = keep.tile([P, PACK], F32, name="minus_half_unit")
         nc.gpsimd.tensor_scalar(minus_half_unit[:], unit_sb[:], -0.5, 0.0, ALU.mult, ALU.add)
 
+        w1w_by_tile = w1w[:].rearrange("p (m t b) -> p t m b", t=PACK, b=2)
         w1w_first = keep.tile([P, 2 * P], U8, name="w1w_first", align_bytes=64)
         w1s_dealt = keep.tile([P, PACK, P], U8, name="w1s_dealt", align_bytes=64)
-        w1w_by_tile = w1w[:].rearrange("p (m t b) -> p t m b", t=PACK, b=2)
-
-        xg_s = keep.tile([P, S], U8, name="xg_s", align_bytes=64)
-        xg_first = keep.tile([P, HALF], U32, name="xg_first", align_bytes=64)
-        halves = [slice(0, HALF), slice(HALF, S)]
-        list_halves = [slice(0, HALF // 16), slice(HALF // 16, S // 16)]
-        nc.vector.tensor_copy(xg_s[:], xs[:].indirect(offs_sb[:]))
+        picked_scales = keep.tile([P, S], U8, name="picked_scales", align_bytes=64)
+        picked_first = keep.tile([P, HALF], U32, name="picked_first", align_bytes=64)
+        nc.vector.tensor_copy(picked_scales[:], xs[:].indirect(offs_sb[:]))
         nc.vector.tensor_copy(out=w1w_first[:].rearrange("p (m b) -> p m b", b=2), in_=w1w_by_tile[:, 0])
-        nc.vector.tensor_copy(xg_first[:], xw[:].indirect(offs_sb[:, list_halves[0]]))
+        nc.vector.tensor_copy(picked_first[:], xw[:].indirect(offs_sb[:, LIST_HALVES[0]]))
         nc.vector.tensor_copy(out=w1s_dealt[:], in_=w1s[:].rearrange("p (m t) -> p t m", t=PACK))
-        xg_second = keep.tile([P, HALF], U32, name="xg_second", tag="w1_bytes", align_bytes=64)
-        nc.vector.tensor_copy(xg_second[:], xw[:].indirect(offs_sb[:, list_halves[1]]))
-        xg_w = [xg_first, xg_second]
-        w1w_rest = keep.tile([P, PACK - 1, 2 * P], U8, name="w1w_rest", tag="x_bytes", align_bytes=64)
+        picked_second = keep.tile([P, HALF], U32, name="picked_second", tag="w1_bytes", align_bytes=64)
+        nc.vector.tensor_copy(picked_second[:], xw[:].indirect(offs_sb[:, LIST_HALVES[1]]))
+        picked_words = [picked_first, picked_second]
+        w1w_rest = keep.tile([P, LAST, 2 * P], U8, name="w1w_rest", tag="x_bytes", align_bytes=64)
         nc.vector.tensor_copy(out=w1w_rest[:].rearrange("p t (m b) -> p t m b", b=2), in_=w1w_by_tile[:, 1:])
-        w1_tiles = [w1w_first[:]] + [w1w_rest[:, t, :] for t in range(PACK - 1)]
+        w1_codes = [w1w_first[:]] + [w1w_rest[:, t, :] for t in range(LAST)]
 
-        heat_win = [keep.tile([P, 2 * S], F32, name=f"heat_win{t}", tag=f"heat_win{t}") for t in range(PACK)]
+        heat_window = [keep.tile([P, 2 * S], F32, name=f"heat_window{t}", tag=f"heat_window{t}") for t in range(PACK)]
         heat = [keep.tile([P, S], F32, name=f"heat{t}") for t in range(PACK)]
         grad = [keep.tile([P, 2, S], F32, name=f"grad{t}") for t in range(PACK)]
         term_div = keep.tile([P, PACK, S], F32, name="term_div")
         term_vx = keep.tile([P, PACK, S], F32, name="term_vx")
 
-        def first_product(bank, t, a):
+        def first_product(bank, t, half):
             nc.tensor.matmul_mx(
                 out=bank,
-                lhsT=w1_tiles[t].bitcast(FP4X4),
+                lhsT=w1_codes[t].bitcast(FP4X4),
                 lhsT_scale=w1s_dealt[:, t, :],
-                rhs=xg_w[a][:].bitcast(FP8X4),
-                rhs_scale=xg_s[:, halves[a]],
+                rhs=picked_words[half][:].bitcast(FP8X4),
+                rhs_scale=picked_scales[:, HALVES[half]],
                 start=True,
                 stop=True,
             )
 
-        def squash(t, cols, bank):
-            nc.scalar.activation(heat_win[t][:, S + cols.start : S + cols.stop], bank, ACT.Tanh)
+        def tanh_of(t, cols):
+            return heat_window[t][:, S + cols.start : S + cols.stop]
 
-        def make_heat(t, cols):
-            nc.scalar.activation(heat_win[t][:, cols], heat_win[t][:, S + cols.start : S + cols.stop], ACT.Exp, scale=0.8)
-            if t < 2:
-                nc.vector.tensor_copy(heat[t][:, cols], heat_win[t][:, cols])
+        def exponential(target, t, cols):
+            nc.scalar.activation(target[:, cols], tanh_of(t, cols), ACT.Exp, scale=0.8)
+
+        for half, cols in enumerate(HALVES):
+            uu = psum.tile([P, HALF], F32, name="uu", tag=("norm0", "second_half")[half])
+            first_product(uu[:], 0, half)
+            nc.scalar.activation(tanh_of(0, cols), uu[:], ACT.Tanh)
+            exponential(heat_window[0], 0, cols)
+            if half == 0:
+                nc.vector.tensor_copy(heat[0][:, cols], heat_window[0][:, cols])
             else:
-                nc.sync.dma_start(out=heat[t][:], in_=heat_win[t][:, :S])
+                exponential(heat[0], 0, cols)
+        for tiles in ((1, 2), (LAST,)):
+            for t in tiles:
+                uu = psum.tile([P, S], F32, name="uu", tag=f"norm{t}")
+                for half, cols in enumerate(HALVES):
+                    first_product(uu[:, cols], t, half)
+                nc.scalar.activation(tanh_of(t, ALL), uu[:], ACT.Tanh)
+            for t in tiles:
+                exponential(heat_window[t], t, ALL)
+                if t == 1:
+                    nc.vector.tensor_copy(heat[t][:], heat_window[t][:, ALL])
+                else:
+                    nc.sync.dma_start(out=heat[t][:], in_=heat_window[t][:, ALL])
 
-        for a in range(2):
-            uu = psum.tile([P, HALF], F32, name="uu", tag=("norm0", "spare")[a])
-            first_product(uu[:], 0, a)
-            squash(0, halves[a], uu[:])
-            make_heat(0, halves[a])
-        for t in range(1, PACK):
-            uu = psum.tile([P, S], F32, name="uu", tag=f"norm{t}")
-            for a in range(2):
-                first_product(uu[:, halves[a]], t, a)
-            squash(t, slice(0, S), uu[:])
-            if t > 1:
-                make_heat(t - 1, slice(0, S))
-        make_heat(PACK - 1, slice(0, S))
+        def difference(t, axis, cols, list_cols):
+            neighbours = (h1_sb, h2_sb)[axis]
+            nc.vector.tensor_tensor(
+                grad[t][:, axis, cols], heat_window[t][:].indirect(neighbours[:, list_cols]), heat[t][:, cols], ALU.subtract
+            )
+
+        for half in range(2):
+            difference(0, 0, HALVES[half], LIST_HALVES[half])
+        for t in range(PACK):
+            for axis in range(2):
+                if (t, axis) != (0, 0):
+                    difference(t, axis, ALL, slice(0, S // GROUP))
 
         def turn(bank, parts):
-            for j in range(PACK):
+            for j in range(S // P):
                 cols = slice(P * j, P * (j + 1))
                 for i, part in enumerate(parts):
                     nc.tensor.matmul(
                         bank[:, cols], part[:, cols], ident[:], start=(i == 0), stop=(i == len(parts) - 1), is_transpose=True
                     )
 
-        st = [{} for t in range(PACK)]
+        square_rows = keep.tile([P, 4, S], F32, name="square_rows")
+        first_square_row = (1, 2, 0, 0)
+        first_guess = keep.tile([P, S], F32, name="first_guess")
+        guess = [first_guess[:]] + [term_vx[:, t, :] for t in range(LAST)]
+        square_sum, guess_squared = [], []
+        for t in range(PACK):
+            squares = square_rows[:, first_square_row[t] : first_square_row[t] + 2, :]
+            nc.scalar.activation(squares, grad[t][:], ACT.Square)
+            square_sum.append(psum.tile([P, S], F32, name="square_sum", tag=f"norm{t}"))
+            turn(square_sum[t], [squares[:, 0, :], squares[:, 1, :]])
+            nc.scalar.activation(guess[t], square_sum[t][:], ACT.Abs_reciprocal_sqrt, bias=0.05)
+            guess_squared.append(keep.tile([P, S], F32, name="guess_squared", tag=f"chain{t}"))
+            nc.scalar.activation(guess_squared[t][:], guess[t], ACT.Square)
 
-        def gradient(t, axis):
-            neighbours = (h1_sb, h2_sb)[axis]
-            nc.vector.tensor_tensor(grad[t][:, axis, :], heat_win[t][:].indirect(neighbours[:]), heat[t][:], ALU.subtract)
+        near_one, inv_norm, grad_sum, unit_sum, fetched, divergence = {}, {}, {}, {}, {}, {}
 
-        def square(t):
-            squares = keep.tile([P, 2, S], F32, name="squares", tag=f"squares{max(t, 1)}")
-            nc.scalar.activation(squares[:], grad[t][:], ACT.Square)
-            sq_sum = psum.tile([P, S], F32, name="sq_sum", tag=f"norm{t}")
-            turn(sq_sum, [squares[:, 0, :], squares[:, 1, :]])
-            st[t]["sq_sum"] = sq_sum
+        def newton_product(t):
+            near_one[t] = keep.tile([P, S], F32, name="near_one", tag=f"near_one{t}")
+            nc.vector.scalar_tensor_tensor(near_one[t][:], square_sum[t][:], 0.05, guess_squared[t][:], ALU.add, ALU.mult)
 
-        def guess_root(t):
-            guess = ring.tile([P, S], F32, name="guess")
-            nc.scalar.activation(guess[:], st[t]["sq_sum"][:], ACT.Abs_reciprocal_sqrt, bias=0.05)
-            st[t]["guess"] = guess
+        def newton_update(t):
+            turned = keep.tile([P, S], F32, name="turned", tag=f"turned{t}" if t else "chain1")
+            nc.vector.scalar_tensor_tensor(turned[:], near_one[t][:], -3.0, guess[t], ALU.add, ALU.mult)
+            inv_norm[t] = psum.tile([P, S], F32, name="inv_norm", tag=f"norm{t}")
+            turn(inv_norm[t], [turned[:]])
 
-        def square_guess(t):
-            guess_sq = ring.tile([P, S], F32, name="guess_sq")
-            nc.scalar.activation(guess_sq[:], st[t]["guess"][:], ACT.Square)
-            st[t]["guess_sq"] = guess_sq
+        def add_differences(t):
+            grad_sum[t] = keep.tile([P, S], F32, name="grad_sum", tag=f"near_one{t}" if t else f"heat_window{LAST}")
+            nc.gpsimd.tensor_tensor(grad_sum[t][:], grad[t][:, 0, :], grad[t][:, 1, :], ALU.add)
 
-        def step_y(t):
-            near_one = keep.tile([P, S], F32, name="near_one", tag=f"near_one{t}")
-            nc.vector.scalar_tensor_tensor(near_one[:], st[t]["sq_sum"][:], 0.05, st[t]["guess_sq"][:], ALU.add, ALU.mult)
-            st[t]["near_one"] = near_one
-
-        def step_r(t):
-            inv_t = ring.tile([P, S], F32, name="inv_t")
-            nc.vector.scalar_tensor_tensor(inv_t[:], st[t]["near_one"][:], -3.0, st[t]["guess"][:], ALU.add, ALU.mult)
-            inv = psum.tile([P, S], F32, name="inv", tag=f"norm{t}")
-            turn(inv, [inv_t[:]])
-            st[t]["inv"] = inv
-
-        def step_p(t):
-            g_sum = keep.tile([P, S], F32, name="g_sum", tag=f"near_one{t}" if t else f"heat_win{PACK - 1}")
-            nc.gpsimd.tensor_tensor(g_sum[:], grad[t][:, 0, :], grad[t][:, 1, :], ALU.add)
-            st[t]["g_sum"] = g_sum
-
-        def step_w(t):
+        def normalise_sum(t):
+            unit_sum[t] = keep.tile([P, S], F32, name="unit_sum", tag=f"chain{t + 1}")
             nc.vector.scalar_tensor_tensor(
-                term_vx[:, t, :], st[t]["inv"][:], quarter_unit[:, t : t + 1], grad[t][:, 0, :], ALU.mult, ALU.mult
+                unit_sum[t][:], inv_norm[t][:], minus_half_unit[:, t : t + 1], grad_sum[t][:], ALU.mult, ALU.mult
             )
 
-        def step_s(t):
-            window = ring.tile([P, S], F32, name="window")
+        def normalise_x(t):
             nc.vector.scalar_tensor_tensor(
-                window[:], st[t]["inv"][:], minus_half_unit[:, t : t + 1], st[t]["g_sum"][:], ALU.mult, ALU.mult
+                term_vx[:, t, :], inv_norm[t][:], quarter_unit[:, t : t + 1], grad[t][:, 0, :], ALU.mult, ALU.mult
             )
-            st[t]["window"] = window
 
-        def step_fetch(t):
-            got = ring.tile([P, S], F32, name="got")
-            for a in range(2):
-                nc.scalar.activation(got[:, halves[a]], st[t]["window"][:].indirect(h3_sb[:, list_halves[a]]), ACT.Copy)
-            st[t]["got"] = got
+        def fetch(t):
+            fetched[t] = keep.tile([P, S], F32, name=f"fetched{t}")
+            for cols, list_cols in zip(HALVES, LIST_HALVES):
+                nc.scalar.activation(fetched[t][:, cols], unit_sum[t][:].indirect(h3_sb[:, list_cols]), ACT.Copy)
 
-        def step_d(t):
-            div = ring.tile([P, S], F32, name="div")
-            nc.vector.tensor_tensor(div[:], st[t]["window"][:], st[t]["got"][:], ALU.subtract)
-            st[t]["div"] = div
+        def subtract_fetched(t):
+            if t in (1, 2):
+                divergence[t] = grad[LAST][:, t - 1, :]
+            else:
+                tag = "last_divergence" if t else f"near_one{LAST}"
+                divergence[t] = keep.tile([P, S], F32, name="divergence", tag=tag)[:]
+            nc.vector.tensor_tensor(divergence[t], unit_sum[t][:], fetched[t][:], ALU.subtract)
 
-        def step_t(t):
-            nc.vector.tensor_tensor(term_div[:, t, :], st[t]["div"][:], heat[t][:], ALU.mult)
+        def weigh_by_heat(t):
+            nc.vector.tensor_tensor(term_div[:, t, :], divergence[t], heat[t][:], ALU.mult)
 
-        gradient(0, 0)
-        gradient(0, 1)
-        gradient(1, 0)
-        gradient(1, 1)
-        square(0)
-        gradient(2, 0)
-        gradient(2, 1)
-        gradient(3, 0)
-        gradient(3, 1)
-        guess_root(0)
-        square(1)
-        square_guess(0)
-        square(2)
-        guess_root(1)
-        square_guess(1)
-        step_p(0)
-        step_y(0)
-        step_y(1)
-        guess_root(2)
-        square(3)
-        square_guess(2)
-        step_r(0)
-        step_r(1)
-        step_p(1)
-        step_y(2)
-        step_s(0)
-        step_w(0)
-        guess_root(3)
-        square_guess(3)
-        step_fetch(0)
-        step_r(2)
-        step_p(2)
-        step_y(3)
-        step_s(1)
-        step_w(1)
-        step_fetch(1)
-        step_r(3)
-        step_p(3)
-        step_s(2)
-        step_w(2)
-        step_fetch(2)
-        step_w(3)
-        step_s(3)
-        step_fetch(3)
-        step_d(0)
-        step_d(1)
-        step_t(0)
-        step_d(2)
-        step_t(1)
-        step_d(3)
-        step_t(2)
-        step_t(3)
+        add_differences(0)
+        newton_product(0)
+        newton_product(1)
+        newton_update(0)
+        for t in range(1, PACK):
+            newton_update(t)
+            add_differences(t)
+            if t < LAST:
+                newton_product(t + 1)
+            normalise_sum(t - 1)
+            normalise_x(t - 1)
+            fetch(t - 1)
+        normalise_x(LAST)
+        normalise_sum(LAST)
+        fetch(LAST)
+        subtract_fetched(0)
+        for t in range(1, PACK):
+            subtract_fetched(t)
+            weigh_by_heat(t - 1)
+        weigh_by_heat(LAST)
 
+        out_by_tile = out.rearrange("(m p) n -> p m n", p=P)
 
-        out_v = out.rearrange("(m p) n -> p m n", p=P)
-
-        def add_terms(c0, width):
-            cols = slice(c0, c0 + width)
-            hid = keep.tile([P, width, PACK], BF16, name=f"hid{c0}", align_bytes=64)
+        def add_terms(start, width):
+            cols = slice(start, start + width)
+            hid = keep.tile([P, width, PACK], BF16, name=f"hid{start}", align_bytes=64)
             nc.vector.tensor_tensor(
                 hid[:].rearrange("p (c i) t -> p c t i", i=2),
                 term_div[:, :, cols].rearrange("p t (c i) -> p c t i", i=2),
@@ -276,15 +256,15 @@ def tile_picked_yheatg_mul_p_kernel(tc, x_words, x_scales, w1_words, w1_scales, 
             )
             return hid
 
-        def quantise(c0, width, hid):
-            codes = keep.tile([P, width], U32, name=f"codes{c0}", align_bytes=64)
-            scales = keep.tile([P, width], U8, name=f"scales{c0}", align_bytes=64)
+        def quantise(start, width, hid):
+            codes = keep.tile([P, width], U32, name=f"codes{start}", align_bytes=64)
+            scales = keep.tile([P, width], U8, name=f"scales{start}", align_bytes=64)
             nc.vector.quantize_mx(out=codes[:].bitcast(FP8X4), scales=scales[:], in_=hid[:].rearrange("p n t -> p (n t)"))
             return codes, scales
 
-        def product(acc, m, codes, scales):
+        def second_product(bank, m, codes, scales):
             nc.tensor.matmul_mx(
-                out=acc,
+                out=bank,
                 lhsT=w2w[:, 2 * P * m : 2 * P * (m + 1)].bitcast(FP4X4),
                 lhsT_scale=w2s[:, P * m : P * (m + 1)],
                 rhs=codes[:].bitcast(FP8X4),
@@ -293,30 +273,27 @@ def tile_picked_yheatg_mul_p_kernel(tc, x_words, x_scales, w1_words, w1_scales, 
                 stop=True,
             )
 
-        def finish(c0, width, hid, bank_tag):
-            codes, scales = quantise(c0, width, hid)
-            acc = psum.tile([P, 2, width], F32, name="acc", tag=bank_tag)
-            for m in range(2):
-                product(acc[:, m, :], m, codes, scales)
-            res = keep.tile([P, 2, width], F32, name=f"res{c0}")
-            nc.scalar.copy(res[:], acc[:])
-            nc.sync.dma_start(out=out_v[:, :, c0 : c0 + width], in_=res[:])
+        def finish(start, width, hid, bank_tag):
+            codes, scales = quantise(start, width, hid)
+            sums = psum.tile([P, N // P, width], F32, name="sums", tag=bank_tag)
+            for m in range(N // P):
+                second_product(sums[:, m, :], m, codes, scales)
+            result = keep.tile([P, N // P, width], F32, name=f"result{start}")
+            nc.scalar.copy(result[:], sums[:])
+            nc.sync.dma_start(out=out_by_tile[:, :, start : start + width], in_=result[:])
 
-        def finish_last(c0, width, hid):
-            codes, scales = quantise(c0, width, hid)
-            for m in range(2):
-                acc = psum.tile([P, width], F32, name="acc", tag=f"norm{2 + m}")
-                product(acc[:], m, codes, scales)
-                res = keep.tile([P, width], F32, name=f"res_last{m}")
-                if m == 0:
-                    nc.scalar.copy(res[:], acc[:])
-                    nc.scalar.dma_start(out=out_v[:, m, c0 : c0 + width], in_=res[:])
-                else:
-                    nc.vector.tensor_copy(res[:], acc[:])
-                    nc.sync.dma_start(out=out_v[:, m, c0 : c0 + width], in_=res[:])
+        def finish_split(start, width, hid):
+            codes, scales = quantise(start, width, hid)
+            ways = (("norm2", nc.scalar.copy, nc.scalar), ("norm3", nc.vector.tensor_copy, nc.sync))
+            for m, (bank_tag, copy_out, queue) in enumerate(ways):
+                sums = psum.tile([P, width], F32, name="sums", tag=bank_tag)
+                second_product(sums[:], m, codes, scales)
+                result = keep.tile([P, width], F32, name=f"last_result{m}")
+                copy_out(result[:], sums[:])
+                queue.dma_start(out=out_by_tile[:, m, start : start + width], in_=result[:])
 
-        first = add_terms(*CHUNKS[0])
-        second = add_terms(*CHUNKS[1])
-        finish(*CHUNKS[0], first, "norm0")
-        finish(*CHUNKS[1], second, "norm1")
-        finish_last(*CHUNKS[2], add_terms(*CHUNKS[2]))
+        wide_hid = add_terms(*WIDE)
+        narrow_hid = add_terms(*NARROW)
+        finish(*WIDE, wide_hid, "norm0")
+        finish(*NARROW, narrow_hid, "norm1")
+        finish_split(*FINAL, add_terms(*FINAL))

from contextlib import ExitStack

import concourse.mybir as mybir
from concourse.masks import make_identity

K, T, S, N, H = 512, 1024, 512, 256, 512
FLOPS = 2 * K * H * S + 2 * H * N * S

F32 = mybir.dt.float32
BF16 = mybir.dt.bfloat16
I32 = mybir.dt.int32
U32 = mybir.dt.uint32
U16 = mybir.dt.uint16
U8 = mybir.dt.uint8
FP8X4 = mybir.dt.float8_e4m3fn_x4
FP4X4 = mybir.dt.float4_e2m1fn_x4
ACT = mybir.ActivationFunctionType
ALU = mybir.AluOpType

P = 128
PACK = 4
LAST = PACK - 1
QUADRANTS = 4
GROUP = 16
HALF = S // 2
HALVES = (slice(0, HALF), slice(HALF, S))
LIST_HALVES = (slice(0, HALF // GROUP), slice(HALF // GROUP, S // GROUP))
ALL = slice(0, S)
WIDE, NARROW, FINAL = (0, 256), (256, 128), (384, 128)


def load_scale_rows(nc, plane, rows):
    for q in range(QUADRANTS):
        nc.sync.dma_start(out=plane[32 * q : 32 * q + 4, :].bitcast(I32), in_=rows[4 * q : 4 * q + 4, :].bitcast(I32))


def load_scale_rows_for_copy(nc, plane, rows):
    words = rows.shape[1] // 4
    for q in range(QUADRANTS):
        four_rows = rows[4 * q : 4 * q + 4, :].bitcast(I32)
        nc.sync.dma_start(
            out=plane[32 * q : 32 * q + 32, :].bitcast(I32), in_=four_rows.unsqueeze(0).to_broadcast([8, 4, words])
        )


def tile_picked_yheatg_mul_p_kernel(
    tc, x_words, x_scales, w1_words, w1_scales, unit, w2_words, w2_scales, offs, h1, h2, h3, out
):
    nc = tc.nc
    with ExitStack() as ctx:
        keep = ctx.enter_context(tc.tile_pool(name="keep", bufs=1))
        psum = ctx.enter_context(tc.psum_pool(name="psum", bufs=1))

        offs_sb = keep.tile([P, S // GROUP], U16, name="offs_sb")
        h1_sb = keep.tile([P, S // GROUP], U16, name="h1_sb")
        h2_sb = keep.tile([P, S // GROUP], U16, name="h2_sb")
        h3_sb = keep.tile([P, S // GROUP], U16, name="h3_sb")
        xw = keep.tile([P, T], U32, name="xw", tag="x_bytes", align_bytes=64)
        xs = keep.tile([P, T], U8, name="xs", align_bytes=64)
        w1w = keep.tile([P, 2 * H], U8, name="w1w", align_bytes=64)
        w1s = keep.tile([P, H], U8, name="w1s", tag="w1_bytes", align_bytes=64)
        w2w = keep.tile([P, 2 * N], U8, name="w2w", align_bytes=64)
        w2s = keep.tile([P, N], U8, name="w2s", align_bytes=64)
        unit_sb = keep.tile([P, PACK], F32, name="unit_sb")
        ident = keep.tile([P, P], F32, name="ident")

        nc.gpsimd.memset(w2s[:].bitcast(I32), 0)
        nc.sync.dma_start(offs_sb[:], offs)
        load_scale_rows_for_copy(nc, xs, x_scales[0])
        nc.sync.dma_start(out=w1w[:].bitcast(I32), in_=w1_words[0].bitcast(I32))
        nc.sync.dma_start(out=xw[:].bitcast(I32), in_=x_words[0].rearrange("p n t -> p (n t)").bitcast(I32))
        load_scale_rows_for_copy(nc, w1s, w1_scales[0])
        nc.sync.dma_start(h1_sb[:], h1)
        nc.sync.dma_start(h2_sb[:], h2)
        nc.sync.dma_start(out=unit_sb[:], in_=unit.rearrange("(p t) o -> p (t o)", t=PACK))
        nc.sync.dma_start(h3_sb[:], h3)
        nc.sync.dma_start(out=w2w[:].bitcast(I32), in_=w2_words[0].bitcast(I32))
        load_scale_rows(nc, w2s, w2_scales[0])
        make_identity(nc, ident[:])

        quarter_unit = keep.tile([P, PACK], F32, name="quarter_unit")
        nc.gpsimd.tensor_scalar(quarter_unit[:], unit_sb[:], 0.25, 0.0, ALU.mult, ALU.add)
        minus_half_unit = keep.tile([P, PACK], F32, name="minus_half_unit")
        nc.gpsimd.tensor_scalar(minus_half_unit[:], unit_sb[:], -0.5, 0.0, ALU.mult, ALU.add)

        w1w_by_tile = w1w[:].rearrange("p (m t b) -> p t m b", t=PACK, b=2)
        w1w_first = keep.tile([P, 2 * P], U8, name="w1w_first", align_bytes=64)
        w1s_dealt = keep.tile([P, PACK, P], U8, name="w1s_dealt", align_bytes=64)
        picked_scales = keep.tile([P, S], U8, name="picked_scales", align_bytes=64)
        picked_first = keep.tile([P, HALF], U32, name="picked_first", align_bytes=64)
        nc.vector.tensor_copy(picked_scales[:], xs[:].indirect(offs_sb[:]))
        nc.vector.tensor_copy(out=w1w_first[:].rearrange("p (m b) -> p m b", b=2), in_=w1w_by_tile[:, 0])
        nc.vector.tensor_copy(picked_first[:], xw[:].indirect(offs_sb[:, LIST_HALVES[0]]))
        nc.vector.tensor_copy(out=w1s_dealt[:], in_=w1s[:].rearrange("p (m t) -> p t m", t=PACK))
        picked_second = keep.tile([P, HALF], U32, name="picked_second", tag="w1_bytes", align_bytes=64)
        nc.vector.tensor_copy(picked_second[:], xw[:].indirect(offs_sb[:, LIST_HALVES[1]]))
        picked_words = [picked_first, picked_second]
        w1w_rest = keep.tile([P, LAST, 2 * P], U8, name="w1w_rest", tag="x_bytes", align_bytes=64)
        nc.vector.tensor_copy(out=w1w_rest[:].rearrange("p t (m b) -> p t m b", b=2), in_=w1w_by_tile[:, 1:])
        w1_codes = [w1w_first[:]] + [w1w_rest[:, t, :] for t in range(LAST)]

        heat_window = [keep.tile([P, 2 * S], F32, name=f"heat_window{t}", tag=f"heat_window{t}") for t in range(PACK)]
        heat = [keep.tile([P, S], F32, name=f"heat{t}") for t in range(PACK)]
        grad = [keep.tile([P, 2, S], F32, name=f"grad{t}") for t in range(PACK)]
        term_div = keep.tile([P, PACK, S], F32, name="term_div")
        term_vx = keep.tile([P, PACK, S], F32, name="term_vx")

        def first_product(bank, t, half):
            nc.tensor.matmul_mx(
                out=bank,
                lhsT=w1_codes[t].bitcast(FP4X4),
                lhsT_scale=w1s_dealt[:, t, :],
                rhs=picked_words[half][:].bitcast(FP8X4),
                rhs_scale=picked_scales[:, HALVES[half]],
                start=True,
                stop=True,
            )

        def tanh_of(t, cols):
            return heat_window[t][:, S + cols.start : S + cols.stop]

        def exponential(target, t, cols):
            nc.scalar.activation(target[:, cols], tanh_of(t, cols), ACT.Exp, scale=0.8)

        for half, cols in enumerate(HALVES):
            uu = psum.tile([P, HALF], F32, name="uu", tag=("norm0", "second_half")[half])
            first_product(uu[:], 0, half)
            nc.scalar.activation(tanh_of(0, cols), uu[:], ACT.Tanh)
            exponential(heat_window[0], 0, cols)
            if half == 0:
                nc.vector.tensor_copy(heat[0][:, cols], heat_window[0][:, cols])
            else:
                exponential(heat[0], 0, cols)
        for tiles in ((1, 2), (LAST,)):
            for t in tiles:
                uu = psum.tile([P, S], F32, name="uu", tag=f"norm{t}")
                for half, cols in enumerate(HALVES):
                    first_product(uu[:, cols], t, half)
                nc.scalar.activation(tanh_of(t, ALL), uu[:], ACT.Tanh)
            for t in tiles:
                exponential(heat_window[t], t, ALL)
                if t == 1:
                    nc.vector.tensor_copy(heat[t][:], heat_window[t][:, ALL])
                else:
                    nc.sync.dma_start(out=heat[t][:], in_=heat_window[t][:, ALL])

        def difference(t, axis, cols, list_cols):
            neighbours = (h1_sb, h2_sb)[axis]
            nc.vector.tensor_tensor(
                grad[t][:, axis, cols], heat_window[t][:].indirect(neighbours[:, list_cols]), heat[t][:, cols], ALU.subtract
            )

        for half in range(2):
            difference(0, 0, HALVES[half], LIST_HALVES[half])
        for t in range(PACK):
            for axis in range(2):
                if (t, axis) != (0, 0):
                    difference(t, axis, ALL, slice(0, S // GROUP))

        def turn(bank, parts):
            for j in range(S // P):
                cols = slice(P * j, P * (j + 1))
                for i, part in enumerate(parts):
                    nc.tensor.matmul(
                        bank[:, cols], part[:, cols], ident[:], start=(i == 0), stop=(i == len(parts) - 1), is_transpose=True
                    )

        square_rows = keep.tile([P, 4, S], F32, name="square_rows")
        first_square_row = (1, 2, 0, 0)
        first_guess = keep.tile([P, S], F32, name="first_guess")
        guess = [first_guess[:]] + [term_vx[:, t, :] for t in range(LAST)]
        square_sum, guess_squared = [], []
        for t in range(PACK):
            squares = square_rows[:, first_square_row[t] : first_square_row[t] + 2, :]
            nc.scalar.activation(squares, grad[t][:], ACT.Square)
            square_sum.append(psum.tile([P, S], F32, name="square_sum", tag=f"norm{t}"))
            turn(square_sum[t], [squares[:, 0, :], squares[:, 1, :]])
            nc.scalar.activation(guess[t], square_sum[t][:], ACT.Abs_reciprocal_sqrt, bias=0.05)
            guess_squared.append(keep.tile([P, S], F32, name="guess_squared", tag=f"chain{t}"))
            nc.scalar.activation(guess_squared[t][:], guess[t], ACT.Square)

        near_one, inv_norm, grad_sum, unit_sum, fetched, divergence = {}, {}, {}, {}, {}, {}

        def newton_product(t):
            near_one[t] = keep.tile([P, S], F32, name="near_one", tag=f"near_one{t}")
            nc.vector.scalar_tensor_tensor(near_one[t][:], square_sum[t][:], 0.05, guess_squared[t][:], ALU.add, ALU.mult)

        def newton_update(t):
            turned = keep.tile([P, S], F32, name="turned", tag=f"turned{t}" if t else "chain1")
            nc.vector.scalar_tensor_tensor(turned[:], near_one[t][:], -3.0, guess[t], ALU.add, ALU.mult)
            inv_norm[t] = psum.tile([P, S], F32, name="inv_norm", tag=f"norm{t}")
            turn(inv_norm[t], [turned[:]])

        def add_differences(t):
            grad_sum[t] = keep.tile([P, S], F32, name="grad_sum", tag=f"near_one{t}" if t else f"heat_window{LAST}")
            nc.gpsimd.tensor_tensor(grad_sum[t][:], grad[t][:, 0, :], grad[t][:, 1, :], ALU.add)

        def normalise_sum(t):
            unit_sum[t] = keep.tile([P, S], F32, name="unit_sum", tag=f"chain{t + 1}")
            nc.vector.scalar_tensor_tensor(
                unit_sum[t][:], inv_norm[t][:], minus_half_unit[:, t : t + 1], grad_sum[t][:], ALU.mult, ALU.mult
            )

        def normalise_x(t):
            nc.vector.scalar_tensor_tensor(
                term_vx[:, t, :], inv_norm[t][:], quarter_unit[:, t : t + 1], grad[t][:, 0, :], ALU.mult, ALU.mult
            )

        def fetch(t):
            fetched[t] = keep.tile([P, S], F32, name=f"fetched{t}")
            for cols, list_cols in zip(HALVES, LIST_HALVES):
                nc.scalar.activation(fetched[t][:, cols], unit_sum[t][:].indirect(h3_sb[:, list_cols]), ACT.Copy)

        def subtract_fetched(t):
            if t in (1, 2):
                divergence[t] = grad[LAST][:, t - 1, :]
            else:
                tag = "last_divergence" if t else f"near_one{LAST}"
                divergence[t] = keep.tile([P, S], F32, name="divergence", tag=tag)[:]
            nc.vector.tensor_tensor(divergence[t], unit_sum[t][:], fetched[t][:], ALU.subtract)

        def weigh_by_heat(t):
            nc.vector.tensor_tensor(term_div[:, t, :], divergence[t], heat[t][:], ALU.mult)

        add_differences(0)
        newton_product(0)
        newton_product(1)
        newton_update(0)
        for t in range(1, PACK):
            newton_update(t)
            add_differences(t)
            if t < LAST:
                newton_product(t + 1)
            normalise_sum(t - 1)
            normalise_x(t - 1)
            fetch(t - 1)
        normalise_x(LAST)
        normalise_sum(LAST)
        fetch(LAST)
        subtract_fetched(0)
        for t in range(1, PACK):
            subtract_fetched(t)
            weigh_by_heat(t - 1)
        weigh_by_heat(LAST)

        out_by_tile = out.rearrange("(m p) n -> p m n", p=P)

        def add_terms(start, width):
            cols = slice(start, start + width)
            hid = keep.tile([P, width, PACK], BF16, name=f"hid{start}", align_bytes=64)
            nc.vector.tensor_tensor(
                hid[:].rearrange("p (c i) t -> p c t i", i=2),
                term_div[:, :, cols].rearrange("p t (c i) -> p c t i", i=2),
                term_vx[:, :, cols].rearrange("p t (c i) -> p c t i", i=2),
                ALU.add,
            )
            return hid

        def quantise(start, width, hid):
            codes = keep.tile([P, width], U32, name=f"codes{start}", align_bytes=64)
            scales = keep.tile([P, width], U8, name=f"scales{start}", align_bytes=64)
            nc.vector.quantize_mx(out=codes[:].bitcast(FP8X4), scales=scales[:], in_=hid[:].rearrange("p n t -> p (n t)"))
            return codes, scales

        def second_product(bank, m, codes, scales):
            nc.tensor.matmul_mx(
                out=bank,
                lhsT=w2w[:, 2 * P * m : 2 * P * (m + 1)].bitcast(FP4X4),
                lhsT_scale=w2s[:, P * m : P * (m + 1)],
                rhs=codes[:].bitcast(FP8X4),
                rhs_scale=scales[:],
                start=True,
                stop=True,
            )

        def finish(start, width, hid, bank_tag):
            codes, scales = quantise(start, width, hid)
            sums = psum.tile([P, N // P, width], F32, name="sums", tag=bank_tag)
            for m in range(N // P):
                second_product(sums[:, m, :], m, codes, scales)
            result = keep.tile([P, N // P, width], F32, name=f"result{start}")
            nc.scalar.copy(result[:], sums[:])
            nc.sync.dma_start(out=out_by_tile[:, :, start : start + width], in_=result[:])

        def finish_split(start, width, hid):
            codes, scales = quantise(start, width, hid)
            ways = (("norm2", nc.scalar.copy, nc.scalar), ("norm3", nc.vector.tensor_copy, nc.sync))
            for m, (bank_tag, copy_out, queue) in enumerate(ways):
                sums = psum.tile([P, width], F32, name="sums", tag=bank_tag)
                second_product(sums[:], m, codes, scales)
                result = keep.tile([P, width], F32, name=f"last_result{m}")
                copy_out(result[:], sums[:])
                queue.dma_start(out=out_by_tile[:, m, start : start + width], in_=result[:])

        wide_hid = add_terms(*WIDE)
        narrow_hid = add_terms(*NARROW)
        finish(*WIDE, wide_hid, "norm0")
        finish(*NARROW, narrow_hid, "norm1")
        finish_split(*FINAL, add_terms(*FINAL))
